import numpy as np
import ml_dtypes


def mxq(x, axis, fmt="e4m3"):
    dtype, down = {"e4m3": (ml_dtypes.float8_e4m3fn, 7), "e5m2": (ml_dtypes.float8_e5m2, 14)}[fmt]
    v = np.moveaxis(np.asarray(x, np.float32).astype(ml_dtypes.bfloat16).astype(np.float64), axis, -1)
    blocks = v.reshape(v.shape[:-1] + (-1, 32))
    amax = np.abs(blocks).max(-1, keepdims=True)
    byte = np.maximum(np.where(amax > 0, np.frexp(amax)[1] - 1 + 127, 0) - down, 1)
    scale = np.exp2(byte - 127.0)
    codes = (blocks / scale).astype(np.float32).astype(dtype).astype(np.float64)
    return np.moveaxis((codes * scale).reshape(v.shape), -1, axis)


WIDE = False


def mx_kscale(k):
    if not WIDE:
        return np.ones(k)
    levels = np.array([10, -10, 5, -5, 0])
    if k % 512:
        return np.exp2(np.random.permutation(np.resize(levels, k // 32))).repeat(32)
    a = np.empty((k // 512, 16))
    for p in range(k // 512):
        a[p, :8] = np.random.permutation(np.resize(levels, 8))
        for g in range(8):
            far = levels[np.abs(levels - a[p, g]) >= 10]
            a[p, g + 8] = far[np.random.randint(len(far))]
    return np.exp2(a.ravel()).repeat(32)


def f64(x):
    return np.asarray(x).astype(np.float64)


def striped(idx):
    return np.tile(idx.reshape(-1, 16).T, (8, 1)).astype(np.uint16)


def unstriped(offs):
    return offs[:16].T.reshape(-1).astype(np.int64)


E2M1 = np.array([0.0, 0.5, 1.0, 1.5, 2.0, 3.0, 4.0, 6.0, -0.0, -0.5, -1.0, -1.5, -2.0, -3.0, -4.0, -6.0])


def pack_weight(w, fmt):
    k, n = w.shape
    w = f64(np.asarray(w, np.float32).astype(ml_dtypes.bfloat16)).reshape(k // 32, 32, n)
    amax = np.abs(w).max(1)
    if fmt == "e4m3":
        byte = np.frexp(amax)[1] - 1 + 127 - 7
    else:
        mant, ex = np.frexp(amax / 6.0)
        byte = np.where(mant > 0.5, ex, ex - 1) + 127
    byte = np.clip(np.where(amax > 0, byte, 1), 1, 254)
    scaled = (w * np.exp2(127.0 - byte)[:, None, :]).reshape(k, n).astype(np.float32)
    by_word = np.ascontiguousarray(scaled.reshape(k // 512, 128, 4, n).transpose(0, 1, 3, 2))
    if fmt == "e4m3":
        words = by_word.astype(ml_dtypes.float8_e4m3fn).view(np.uint8)
    else:
        c = by_word.astype(ml_dtypes.float4_e2m1fn).view(np.uint8) & 0xF
        words = (c[..., 0::2] | (c[..., 1::2] << 4)).reshape(k // 512, 128, 2 * n)
    return np.ascontiguousarray(words), np.ascontiguousarray(byte.astype(np.uint8).reshape(k // 512, 16, n))


def unpack_weight(words, scales, fmt):
    g, _, n = scales.shape
    words = np.ascontiguousarray(words).reshape(g, 128, n, -1)
    if fmt == "e4m3":
        vals = words.view(ml_dtypes.float8_e4m3fn).astype(np.float64)
    else:
        nib = np.empty((g, 128, n, 4), np.uint8)
        nib[..., 0::2] = words & 0xF
        nib[..., 1::2] = words >> 4
        vals = E2M1[nib]
    vals = vals * np.repeat(np.exp2(scales.astype(np.float64) - 127.0), 8, axis=1)[..., None]
    return vals.transpose(0, 1, 3, 2).reshape(g * 512, n)


def gelu(v):
    return 0.5 * v * (1.0 + np.tanh(np.sqrt(2.0 / np.pi) * (v + 0.044715 * v**3)))


def bf(x):
    return np.asarray(x, np.float32).astype(ml_dtypes.bfloat16)


def planes(Y):
    n, m = Y.shape
    b = f64(bf(Y)).reshape(n // 32, 32, m)
    amax = np.abs(b).max(1)
    byte = np.clip(np.where(amax > 0, np.frexp(amax)[1] - 1 + 127 - 7, 1), 1, 254)
    codes = (b * np.exp2(127.0 - byte)[:, None, :]).reshape(n, m).astype(np.float32).astype(ml_dtypes.float8_e4m3fn).view(np.uint8)
    words = codes.reshape(n // 512, 128, 4, m).transpose(0, 1, 3, 2)
    return np.ascontiguousarray(words), np.ascontiguousarray(byte.astype(np.uint8).reshape(n // 512, 16, m))


K, T, S, P, H, N = 1024, 4096, 1024, 512, 1024, 512

def setup_inputs():
    n = np.random.standard_normal
    s = mx_kscale(K)[:, None]
    u = mx_kscale(H)[:, None]
    d = {}
    d["tab_words"], d["tab_scales"] = pack_weight(n((K, T)) * s, "e2m1")
    d["offs"] = striped(np.random.permutation(T)[:S])
    d["pos1"] = striped(np.random.permutation(S)[:P])
    d["pos2"] = striped(np.random.permutation(S)[:P])
    d["w1_words"], d["w1_scales"] = pack_weight(2.0 * n((K, H)) / K**0.5 / s, "e4m3")
    d["gain"] = (np.exp(0.3 * n(H)) * u[:, 0]).astype(np.float32)
    wn = 3.0 * n((H, N)) / H**0.5 / u * np.exp(0.8 * n(N))[None, :]
    d["wn_words"], d["wn_scales"] = pack_weight(wn, "e2m1")
    d["wd"] = (4.0 * n((H, N)) / H**0.5 / u).astype(np.float32)
    return d

def reference(tab_words, tab_scales, offs, pos1, pos2, w1_words, w1_scales, gain, wn_words, wn_scales, wd):
    v = unpack_weight(tab_words, tab_scales, "e2m1")[:, unstriped(offs)]
    w1 = unpack_weight(w1_words, w1_scales, "e4m3")
    wn = unpack_weight(wn_words, wn_scales, "e2m1")
    a = w1.T @ v
    h = 1.0 / (1.0 + np.exp(-a))
    hg = f64(gain)[:, None] * h
    z = hg[:, unstriped(pos1)] * h[:, unstriped(pos2)]
    zq = mxq(z, 0, "e4m3")
    top = wn.T @ zq
    low = mxq(f64(wd), 0, "e4m3").T @ zq
    y = top / (1.0 + np.abs(low))
    words, scales = planes(y)
    return y, words, scales

@@ -1,0 +1,318 @@
+from contextlib import ExitStack
+
+import concourse.mybir as mybir
+
+F32 = mybir.dt.float32
+BF16 = mybir.dt.bfloat16
+I32 = mybir.dt.int32
+U32 = mybir.dt.uint32
+U16 = mybir.dt.uint16
+U8 = mybir.dt.uint8
+FP8X4 = mybir.dt.float8_e4m3fn_x4
+FP4X4 = mybir.dt.float4_e2m1fn_x4
+ACT = mybir.ActivationFunctionType
+MULT = mybir.AluOpType.mult
+
+K, T, S, NP, H, N = 1024, 4096, 1024, 512, 1024, 512
+P = 128
+PACK = 4
+BANK = 512
+FLOPS = 2 * K * H * S + 2 * 2 * H * N * NP
+
+CHUNKS = ((0, 256), (256, 128), (384, 128))
+WIDEST = 256
+PLANE_COLS = S + H + N
+
+
+def tile_list_flake_overlap_features_kernel(
+    tc, tab_words, tab_scales, offs, pos1, pos2, w1_words, w1_scales, gain, wn_words, wn_scales, wd,
+    out_0, out_1, out_2,
+):
+    nc = tc.nc
+    with ExitStack() as ctx:
+        lists = ctx.enter_context(tc.tile_pool(name="lists", bufs=1))
+        keep = ctx.enter_context(tc.tile_pool(name="keep", bufs=1))
+        ring = ctx.enter_context(tc.tile_pool(name="ring", bufs=3))
+        psum = ctx.enter_context(tc.psum_pool(name="psum", bufs=1))
+
+        def held(shape, dtype, name, tag=None):
+            return keep.tile(shape, dtype, name=name, tag=tag or name, align_bytes=64)
+
+        banks = [psum.tile([P, BANK], F32, name=f"bank{i}") for i in range(8)]
+
+        offs_sb = lists.tile([P, S // 16], U16, name="offs_sb")
+        pos1_sb = lists.tile([P, NP // 16], U16, name="pos1_sb")
+        pos2_sb = lists.tile([P, NP // 16], U16, name="pos2_sb")
+
+        tab_scale_rows = held([P, T], U8, "tab_scale_rows")
+        tab_word_rows = [held([P, T], U16, f"tab_word_rows{a}") for a in range(2)]
+        weight_scale_rows = held([P, H + N], U8, "weight_scale_rows")
+        gain_sb = held([P, 2, PACK], F32, "gain_sb")
+        planes = [held([P, PLANE_COLS], U8, f"planes{a}") for a in range(2)]
+
+        for rows in (tab_scale_rows, weight_scale_rows):
+            nc.vector.memset(rows[32:64, :].bitcast(I32), 0)
+            nc.vector.memset(rows[64:128, :].bitcast(I32), 0)
+        nc.gpsimd.memset(planes[1][:].bitcast(I32), 0)
+
+        def load_w1(b):
+            raw = held([P, 2, 512], U32, f"w1_raw{b}", "w1_raw")
+            nc.sync.dma_start(
+                out=raw[:].bitcast(I32),
+                in_=w1_words.rearrange("a p c i -> p a (c i)")[:, :, 2048 * b : 2048 * (b + 1)].bitcast(I32),
+            )
+            return raw
+
+        nc.sync.dma_start(out=offs_sb[:], in_=offs)
+        nc.scalar.dma_start(out=gain_sb[:], in_=gain.rearrange("(b p i) -> p b i", b=2, i=PACK))
+        nc.sync.dma_start(
+            out=tab_scale_rows[0:32, :].bitcast(I32), in_=tab_scales.rearrange("a q t -> (a q) t").bitcast(I32)
+        )
+        nc.sync.dma_start(
+            out=weight_scale_rows[0:32, 0:H].bitcast(I32), in_=w1_scales.rearrange("a q c -> (a q) c").bitcast(I32)
+        )
+        nc.sync.dma_start(
+            out=weight_scale_rows[0:32, H : H + N].bitcast(I32),
+            in_=wn_scales.rearrange("a q c -> (a q) c").bitcast(I32),
+        )
+        nc.sync.dma_start(out=tab_word_rows[0][:].bitcast(I32), in_=tab_words[0].bitcast(I32))
+        w1_raw = load_w1(0)
+        nc.sync.dma_start(out=pos1_sb[:], in_=pos1)
+        nc.sync.dma_start(out=pos2_sb[:], in_=pos2)
+        nc.sync.dma_start(out=tab_word_rows[1][:].bitcast(I32), in_=tab_words[1].bitcast(I32))
+
+        gain_wide = held([P, 8, WIDEST], F32, "gain_wide")
+        nc.scalar.copy(
+            out=gain_wide[:],
+            in_=gain_sb[:].rearrange("p b i -> p (b i)").unsqueeze(2).to_broadcast([P, 8, WIDEST]),
+        )
+
+        picked_scales = held([P, S], U8, "picked_scales")
+        nc.vector.tensor_copy(out=picked_scales[:], in_=tab_scale_rows[:].indirect(offs_sb[:]))
+        nc.vector.tensor_copy(
+            out=planes[0][:, S:PLANE_COLS].rearrange("p (g i q) -> p g i q", i=PACK, q=P),
+            in_=weight_scale_rows[:].rearrange("p (g q i) -> p g i q", i=PACK, q=P),
+        )
+        nc.vector.tensor_copy(out=planes[0][:, 0:S].bitcast(I32), in_=picked_scales[:].bitcast(I32))
+        for a in range(2):
+            for q in range(1 - a, 4):
+                row = 16 * a + 4 * q
+                nc.scalar.dma_start(
+                    out=planes[a][32 * q : 32 * q + 4, :].bitcast(I32),
+                    in_=planes[0][row : row + 4, :].bitcast(I32),
+                )
+        v_words = [[held([P, BANK], U16, f"v_words{a}{half}") for half in range(2)] for a in range(2)]
+        wd_raw = []
+        for a in range(2):
+            for half in range(2):
+                nc.vector.tensor_copy(
+                    out=v_words[a][half][:],
+                    in_=tab_word_rows[a][:].indirect(offs_sb[:, 32 * half : 32 * (half + 1)]),
+                )
+
+        w1_codes = [[held([P, PACK, P], U32, f"w1_codes{a}{b}") for b in range(2)] for a in range(2)]
+
+        def deal_w1(b, raw):
+            for a in range(2):
+                nc.scalar.copy(
+                    out=w1_codes[a][b][:].rearrange("p i q -> p q i"),
+                    in_=raw[:, a, :].rearrange("p (q i) -> p q i", i=PACK),
+                )
+
+        h_rows = [held([P, S], F32, f"h_rows{r}") for r in range(8)]
+
+        def first_pass(r, half, a):
+            b, i = divmod(r, PACK)
+            cols = slice(BANK * half, BANK * (half + 1))
+            nc.tensor.matmul_mx(
+                out=banks[2 * i + half][:],
+                lhsT=w1_codes[a][b][:, i, :].bitcast(FP8X4),
+                lhsT_scale=planes[a][:, S + P * r : S + P * (r + 1)],
+                rhs=v_words[a][half][:].bitcast(FP4X4),
+                rhs_scale=planes[a][:, cols],
+                start=(a == 0),
+                stop=(a == 1),
+            )
+
+        def sigmoid(r, half):
+            nc.scalar.activation(
+                out=h_rows[r][:, BANK * half : BANK * (half + 1)], in_=banks[2 * (r % PACK) + half][:], func=ACT.Sigmoid
+            )
+
+        deal_w1(0, w1_raw)
+        w1_raw = load_w1(1)
+        for b in range(2):
+            raw = held([P, PACK, N], F32, f"wd_raw{b}", f"tab_word_rows{b}")
+            nc.sync.dma_start(out=raw[:], in_=wd[512 * b : 512 * (b + 1), :].rearrange("(p i) n -> p i n", i=PACK))
+            wd_raw.append(raw)
+        for half in range(2):
+            for r in range(PACK):
+                first_pass(r, half, 0)
+        for r in range(PACK):
+            for half in range(2):
+                first_pass(r, half, 1)
+                sigmoid(r, half)
+            if r == 1:
+                deal_w1(1, w1_raw)
+        for r in range(PACK, 2 * PACK):
+            for half in range(2):
+                first_pass(r, half, 0)
+                first_pass(r, half, 1)
+                sigmoid(r, half)
+
+        wn_raw = held([P, 2, N], U16, "wn_raw", "w1_raw")
+        nc.sync.dma_start(out=wn_raw[:].bitcast(I32), in_=wn_words.rearrange("a p c -> p a c").bitcast(I32))
+        wn_codes = held([P, 2, PACK, P], U16, "wn_codes")
+        wd_codes = [held([P, N], U32, f"wd_codes{b}") for b in range(2)]
+        wd_planes = [held([P, N], U8, f"wd_planes{b}") for b in range(2)]
+        wd_round = [held([P, PACK, P, PACK], BF16, f"wd_round{b}") for b in range(2)]
+
+        def round_wd(b):
+            dst = wd_round[b][:].rearrange("p t q i -> p q i t")
+            src = wd_raw[b][:].rearrange("p i (q t) -> p q i t", t=PACK)
+            nc.scalar.copy(out=dst, in_=src)
+
+        def quantize_wd(b):
+            nc.vector.quantize_mx(
+                out=wd_codes[b][:].bitcast(FP8X4),
+                scales=wd_planes[b][:],
+                in_=wd_round[b][:].rearrange("p t q i -> p (t q i)"),
+            )
+
+        def weave(engine_copy, dst, src):
+            engine_copy(
+                out=dst.rearrange("p (c n) t -> p c t n", n=4),
+                in_=src.rearrange("p t (c n) -> p c t n", n=4),
+            )
+
+        z_rows = {}
+        z_tags = {(1, 1): "wd_round0", (2, 0): "wd_round1"}
+        z_round = [[held([P, w, PACK], BF16, f"z_round{c}{b}") for b in range(2)] for c, (j0, w) in enumerate(CHUNKS)]
+        z_codes = [[held([P, w], U32, f"z_codes{c}{b}") for b in range(2)] for c, (j0, w) in enumerate(CHUNKS)]
+        z_planes = [[held([P, w], U8, f"z_planes{c}{b}") for b in range(2)] for c, (j0, w) in enumerate(CHUNKS)]
+        y_planes = held([P, NP], U8, "y_planes")
+        low_banks = (banks[4:6], banks[0:1], banks[2:3])
+        top_banks = (banks[6:8], banks[1:2], banks[3:4])
+
+        def pick_upper(c, r):
+            j0, w = CHUNKS[c]
+            upper = ring.tile([P, WIDEST], F32, name="upper", align_bytes=64)
+            nc.vector.tensor_tensor(
+                out=upper[:, 0:w],
+                in0=h_rows[r][:].indirect(pos1_sb[:, j0 // 16 : (j0 + w) // 16]),
+                in1=gain_wide[:, r, 0:w],
+                op=MULT,
+            )
+            return upper
+
+        def pick_lower(c, r, upper):
+            j0, w = CHUNKS[c]
+            b, i = divmod(r, PACK)
+            if i == 0:
+                z_rows[c, b] = held([P, PACK, w], F32, f"z_rows{c}{b}", z_tags.get((c, b)))
+            nc.vector.tensor_tensor(
+                out=z_rows[c, b][:, i, :],
+                in0=h_rows[r][:].indirect(pos2_sb[:, j0 // 16 : (j0 + w) // 16]),
+                in1=upper[:, 0:w],
+                op=MULT,
+            )
+
+        def sum_columns(bank_list, w, t):
+            per_bank = BANK // w
+            return bank_list[t // per_bank][:, (t % per_bank) * w : (t % per_bank + 1) * w]
+
+        def second_stage(c, b):
+            j0, w = CHUNKS[c]
+            per_bank = BANK // w
+            nc.vector.quantize_mx(
+                out=z_codes[c][b][:].bitcast(FP8X4),
+                scales=z_planes[c][b][:],
+                in_=z_round[c][b][:].rearrange("p j t -> p (j t)"),
+            )
+            for t in range(PACK):
+                nc.tensor.matmul_mx(
+                    out=sum_columns(low_banks[c], w, t),
+                    lhsT=wd_codes[b][:, P * t : P * (t + 1)].bitcast(FP8X4),
+                    lhsT_scale=wd_planes[b][:, P * t : P * (t + 1)],
+                    rhs=z_codes[c][b][:].bitcast(FP8X4),
+                    rhs_scale=z_planes[c][b][:],
+                    start=(b == 0 and t % per_bank == 0),
+                    stop=(b == 1 and t % per_bank == per_bank - 1),
+                )
+            for t in range(PACK):
+                nc.tensor.matmul_mx(
+                    out=sum_columns(top_banks[c], w, t),
+                    lhsT=wn_codes[:, b, t, :].bitcast(FP4X4),
+                    lhsT_scale=planes[b][:, S + H + P * t : S + H + P * (t + 1)],
+                    rhs=z_codes[c][b][:].bitcast(FP8X4),
+                    rhs_scale=z_planes[c][b][:],
+                    start=(b == 0 and t % per_bank == 0),
+                    stop=(b == 1 and t % per_bank == per_bank - 1),
+                )
+
+        def finish(c):
+            j0, w = CHUNKS[c]
+            last = c == len(CHUNKS) - 1
+            size = held([P, PACK * w], F32, f"size{c}")
+            root = held([P, PACK * w], F32, f"root{c}")
+            damp = held([P, PACK * w], F32, f"damp{c}")
+            y_rows = held([P, PACK, w], F32, f"y_rows{c}")
+            y_round = held([P, w, PACK], BF16, f"y_round{c}")
+            y_codes = held([P, w], U32, f"y_codes{c}")
+            y_flat = y_rows[:].rearrange("p t j -> p (t j)")
+            for k in range(len(low_banks[c])):
+                cols = slice(BANK * k, BANK * (k + 1))
+                nc.scalar.activation(out=size[:, cols], in_=low_banks[c][k][:], func=ACT.Abs)
+                nc.scalar.activation(out=root[:, cols], in_=size[:, cols], func=ACT.Abs_reciprocal_sqrt, bias=1.0)
+                nc.scalar.activation(out=damp[:, cols], in_=root[:, cols], func=ACT.Square)
+                nc.vector.tensor_tensor(out=y_flat[:, cols], in0=top_banks[c][k][:], in1=damp[:, cols], op=MULT)
+            nc.sync.dma_start(
+                out=out_0.rearrange("(p t) j -> p t j", t=PACK)[:, :, j0 : j0 + w], in_=y_rows[:]
+            )
+            weave(nc.vector.tensor_copy if last else nc.scalar.copy, y_round[:], y_rows[:])
+            nc.vector.quantize_mx(
+                out=y_codes[:].bitcast(FP8X4),
+                scales=y_planes[:, j0 : j0 + w],
+                in_=y_round[:].rearrange("p j t -> p (j t)"),
+            )
+            nc.sync.dma_start(
+                out=out_1[0].rearrange("p m t -> p (m t)")[:, 4 * j0 : 4 * (j0 + w)].bitcast(I32),
+                in_=y_codes[:].bitcast(I32),
+            )
+
+        round_wd(0)
+        quantize_wd(0)
+        round_wd(1)
+        quantize_wd(1)
+        nc.scalar.copy(out=wn_codes[:], in_=wn_raw[:].rearrange("p b (q t) -> p b t q", t=PACK))
+        steps = [(c, r) for c in range(len(CHUNKS)) for r in range(8)]
+
+        def after_pick(n, phase):
+            c, r = steps[n]
+            b = r // PACK
+            if r % PACK == PACK - 1:
+                if phase == 0:
+                    weave(nc.vector.tensor_copy, z_round[c][b][:], z_rows[c, b][:])
+                else:
+                    second_stage(c, b)
+                    if b == 1:
+                        finish(c)
+
+        uppers = [pick_upper(*steps[0])]
+        for n, (c, r) in enumerate(steps):
+            if n + 1 < len(steps):
+                uppers.append(pick_upper(*steps[n + 1]))
+            pick_lower(c, r, uppers[n])
+            if n >= 1:
+                after_pick(n - 1, 0)
+            if n >= 2:
+                after_pick(n - 2, 1)
+        after_pick(len(steps) - 1, 0)
+        after_pick(len(steps) - 1, 1)
+
+        for q in range(4):
+            queue = nc.scalar if q % 2 else nc.sync
+            queue.dma_start(
+                out=out_2[0, 4 * q : 4 * q + 4, :].bitcast(I32),
+                in_=y_planes[32 * q : 32 * q + 4, :].bitcast(I32),
+            )

@@ -50,9 +50,10 @@ def tile_list_flake_overlap_features_kernel(
         gain_sb = held([P, 2, PACK], F32, "gain_sb")
         planes = [held([P, PLANE_COLS], U8, f"planes{a}") for a in range(2)]
 
-        for rows in (tab_scale_rows, weight_scale_rows):
-            nc.vector.memset(rows[32:64, :].bitcast(I32), 0)
-            nc.vector.memset(rows[64:128, :].bitcast(I32), 0)
+        nc.vector.memset(tab_scale_rows[32:64, :].bitcast(I32), 0)
+        nc.gpsimd.memset(tab_scale_rows[64:128, :].bitcast(I32), 0)
+        nc.vector.memset(weight_scale_rows[32:64, :].bitcast(I32), 0)
+        nc.gpsimd.memset(weight_scale_rows[64:128, :].bitcast(I32), 0)
         nc.gpsimd.memset(planes[1][:].bitcast(I32), 0)
 
         def load_w1(b):
@@ -81,6 +82,8 @@ def tile_list_flake_overlap_features_kernel(
         nc.sync.dma_start(out=pos2_sb[:], in_=pos2)
         nc.sync.dma_start(out=tab_word_rows[1][:].bitcast(I32), in_=tab_words[1].bitcast(I32))
 
+        warm = held([P, 1], F32, "warm")
+        nc.scalar.activation(out=warm[:], in_=gain_sb[:, 0, 0:1], func=ACT.Sigmoid)
         gain_wide = held([P, 8, WIDEST], F32, "gain_wide")
         nc.scalar.copy(
             out=gain_wide[:],
@@ -89,7 +92,7 @@ def tile_list_flake_overlap_features_kernel(
 
         picked_scales = held([P, S], U8, "picked_scales")
         nc.vector.tensor_copy(out=picked_scales[:], in_=tab_scale_rows[:].indirect(offs_sb[:]))
-        nc.vector.tensor_copy(
+        nc.gpsimd.tensor_copy(
             out=planes[0][:, S:PLANE_COLS].rearrange("p (g i q) -> p g i q", i=PACK, q=P),
             in_=weight_scale_rows[:].rearrange("p (g q i) -> p g i q", i=PACK, q=P),
         )
@@ -97,7 +100,7 @@ def tile_list_flake_overlap_features_kernel(
         for a in range(2):
             for q in range(1 - a, 4):
                 row = 16 * a + 4 * q
-                nc.scalar.dma_start(
+                nc.sync.dma_start(
                     out=planes[a][32 * q : 32 * q + 4, :].bitcast(I32),
                     in_=planes[0][row : row + 4, :].bitcast(I32),
                 )
@@ -110,10 +113,11 @@ def tile_list_flake_overlap_features_kernel(
                     in_=tab_word_rows[a][:].indirect(offs_sb[:, 32 * half : 32 * (half + 1)]),
                 )
 
-        w1_codes = [[held([P, PACK, P], U32, f"w1_codes{a}{b}") for b in range(2)] for a in range(2)]
+        w1_codes = [[None, None], [None, None]]
 
         def deal_w1(b, raw):
             for a in range(2):
+                w1_codes[a][b] = held([P, PACK, P], U32, f"w1_codes{a}{b}", f"w1_codes{a}")
                 nc.scalar.copy(
                     out=w1_codes[a][b][:].rearrange("p i q -> p q i"),
                     in_=raw[:, a, :].rearrange("p (q i) -> p q i", i=PACK),
@@ -140,34 +144,29 @@ def tile_list_flake_overlap_features_kernel(
             )
 
         deal_w1(0, w1_raw)
-        w1_raw = load_w1(1)
         for b in range(2):
-            raw = held([P, PACK, N], F32, f"wd_raw{b}", f"tab_word_rows{b}")
+            if b == 1:
+                w1_raw = load_w1(1)
+            raw = held([P, PACK, N], F32, f"wd_raw{b}", ("picked_scales", "tab_word_rows1")[b])
             nc.sync.dma_start(out=raw[:], in_=wd[512 * b : 512 * (b + 1), :].rearrange("(p i) n -> p i n", i=PACK))
             wd_raw.append(raw)
-        for half in range(2):
-            for r in range(PACK):
-                first_pass(r, half, 0)
-        for r in range(PACK):
+        for r in range(2 * PACK):
             for half in range(2):
+                first_pass(r, half, 0)
                 first_pass(r, half, 1)
                 sigmoid(r, half)
-            if r == 1:
+            if r == PACK - 1:
                 deal_w1(1, w1_raw)
-        for r in range(PACK, 2 * PACK):
-            for half in range(2):
-                first_pass(r, half, 0)
-                first_pass(r, half, 1)
-                sigmoid(r, half)
 
         wn_raw = held([P, 2, N], U16, "wn_raw", "w1_raw")
         nc.sync.dma_start(out=wn_raw[:].bitcast(I32), in_=wn_words.rearrange("a p c -> p a c").bitcast(I32))
         wn_codes = held([P, 2, PACK, P], U16, "wn_codes")
         wd_codes = [held([P, N], U32, f"wd_codes{b}") for b in range(2)]
         wd_planes = [held([P, N], U8, f"wd_planes{b}") for b in range(2)]
-        wd_round = [held([P, PACK, P, PACK], BF16, f"wd_round{b}") for b in range(2)]
+        wd_round = [None, None]
 
         def round_wd(b):
+            wd_round[b] = held([P, PACK, P, PACK], BF16, f"wd_round{b}", ("w1_codes0", "w1_codes1")[b])
             dst = wd_round[b][:].rearrange("p t q i -> p q i t")
             src = wd_raw[b][:].rearrange("p i (q t) -> p q i t", t=PACK)
             nc.scalar.copy(out=dst, in_=src)
@@ -186,7 +185,7 @@ def tile_list_flake_overlap_features_kernel(
             )
 
         z_rows = {}
-        z_tags = {(1, 1): "wd_round0", (2, 0): "wd_round1"}
+        z_tags = {(1, 0): "w1_codes0", (1, 1): "w1_codes1"}
         z_round = [[held([P, w, PACK], BF16, f"z_round{c}{b}") for b in range(2)] for c, (j0, w) in enumerate(CHUNKS)]
         z_codes = [[held([P, w], U32, f"z_codes{c}{b}") for b in range(2)] for c, (j0, w) in enumerate(CHUNKS)]
         z_planes = [[held([P, w], U8, f"z_planes{c}{b}") for b in range(2)] for c, (j0, w) in enumerate(CHUNKS)]
@@ -221,14 +220,16 @@ def tile_list_flake_overlap_features_kernel(
             per_bank = BANK // w
             return bank_list[t // per_bank][:, (t % per_bank) * w : (t % per_bank + 1) * w]
 
-        def second_stage(c, b):
-            j0, w = CHUNKS[c]
-            per_bank = BANK // w
+        def quantize_z(c, b):
             nc.vector.quantize_mx(
                 out=z_codes[c][b][:].bitcast(FP8X4),
                 scales=z_planes[c][b][:],
                 in_=z_round[c][b][:].rearrange("p j t -> p (j t)"),
             )
+
+        def second_stage(c, b):
+            j0, w = CHUNKS[c]
+            per_bank = BANK // w
             for t in range(PACK):
                 nc.tensor.matmul_mx(
                     out=sum_columns(low_banks[c], w, t),
@@ -253,37 +254,61 @@ def tile_list_flake_overlap_features_kernel(
         def finish(c):
             j0, w = CHUNKS[c]
             last = c == len(CHUNKS) - 1
-            size = held([P, PACK * w], F32, f"size{c}")
-            root = held([P, PACK * w], F32, f"root{c}")
-            damp = held([P, PACK * w], F32, f"damp{c}")
-            y_rows = held([P, PACK, w], F32, f"y_rows{c}")
-            y_round = held([P, w, PACK], BF16, f"y_round{c}")
-            y_codes = held([P, w], U32, f"y_codes{c}")
-            y_flat = y_rows[:].rearrange("p t j -> p (t j)")
-            for k in range(len(low_banks[c])):
-                cols = slice(BANK * k, BANK * (k + 1))
-                nc.scalar.activation(out=size[:, cols], in_=low_banks[c][k][:], func=ACT.Abs)
-                nc.scalar.activation(out=root[:, cols], in_=size[:, cols], func=ACT.Abs_reciprocal_sqrt, bias=1.0)
-                nc.scalar.activation(out=damp[:, cols], in_=root[:, cols], func=ACT.Square)
-                nc.vector.tensor_tensor(out=y_flat[:, cols], in0=top_banks[c][k][:], in1=damp[:, cols], op=MULT)
-            nc.sync.dma_start(
-                out=out_0.rearrange("(p t) j -> p t j", t=PACK)[:, :, j0 : j0 + w], in_=y_rows[:]
-            )
-            weave(nc.vector.tensor_copy if last else nc.scalar.copy, y_round[:], y_rows[:])
-            nc.vector.quantize_mx(
-                out=y_codes[:].bitcast(FP8X4),
-                scales=y_planes[:, j0 : j0 + w],
-                in_=y_round[:].rearrange("p j t -> p (j t)"),
-            )
-            nc.sync.dma_start(
-                out=out_1[0].rearrange("p m t -> p (m t)")[:, 4 * j0 : 4 * (j0 + w)].bitcast(I32),
-                in_=y_codes[:].bitcast(I32),
-            )
+            per_bank = BANK // w
+            if last:
+                parts = [(0, 0, PACK, (w // 2) * u, w // 2) for u in range(2)]
+            else:
+                parts = [(k, per_bank * k, per_bank, 0, w) for k in range(len(low_banks[c]))]
+            groups = [[0], [1]] if last else [list(range(len(parts)))]
+
+            def sums(bank_list, part):
+                k, t0, nt, c0, nc_ = part
+                return bank_list[k][:].rearrange("p (t j) -> p t j", j=w)[:, :, c0 : c0 + nc_]
+
+            size = [held([P, p[2], p[4]], F32, f"size{c}{u}") for u, p in enumerate(parts)]
+            root = [held([P, p[2], p[4]], F32, f"root{c}{u}") for u, p in enumerate(parts)]
+            damp = [held([P, p[2], p[4]], F32, f"damp{c}{u}") for u, p in enumerate(parts)]
+            for u, part in enumerate(parts):
+                nc.scalar.activation(out=size[u][:], in_=sums(low_banks[c], part), func=ACT.Abs)
+            for u, part in enumerate(parts):
+                nc.scalar.activation(out=root[u][:], in_=size[u][:], func=ACT.Abs_reciprocal_sqrt, bias=1.0)
+            for u, part in enumerate(parts):
+                nc.scalar.activation(out=damp[u][:], in_=root[u][:], func=ACT.Square)
+            y_rows = []
+            for g, members in enumerate(groups):
+                width = parts[members[0]][4]
+                rows = held([P, PACK, width], F32, f"y_rows{c}{g}")
+                y_rows.append(rows)
+                for u in members:
+                    k, t0, nt, c0, nc_ = parts[u]
+                    nc.vector.tensor_tensor(
+                        out=rows[:, t0 : t0 + nt, :], in0=sums(top_banks[c], parts[u]), in1=damp[u][:], op=MULT
+                    )
+                first = j0 + parts[members[0]][3]
+                nc.sync.dma_start(
+                    out=out_0.rearrange("(p t) j -> p t j", t=PACK)[:, :, first : first + width], in_=rows[:]
+                )
+            y_round = []
+            for g, members in enumerate(groups):
+                width = parts[members[0]][4]
+                y_round.append(held([P, width, PACK], BF16, f"y_round{c}{g}"))
+                weave(nc.vector.tensor_copy if last else nc.scalar.copy, y_round[g][:], y_rows[g][:])
+            for g, members in enumerate(groups):
+                width = parts[members[0]][4]
+                first = j0 + parts[members[0]][3]
+                y_codes = held([P, width], U32, f"y_codes{c}{g}")
+                nc.vector.quantize_mx(
+                    out=y_codes[:].bitcast(FP8X4),
+                    scales=y_planes[:, first : first + width],
+                    in_=y_round[g][:].rearrange("p j t -> p (j t)"),
+                )
+                nc.sync.dma_start(
+                    out=out_1[0].rearrange("p m t -> p (m t)")[:, 4 * first : 4 * (first + width)].bitcast(I32),
+                    in_=y_codes[:].bitcast(I32),
+                )
 
         round_wd(0)
-        quantize_wd(0)
         round_wd(1)
-        quantize_wd(1)
         nc.scalar.copy(out=wn_codes[:], in_=wn_raw[:].rearrange("p b (q t) -> p b t q", t=PACK))
         steps = [(c, r) for c in range(len(CHUNKS)) for r in range(8)]
 
@@ -294,14 +319,21 @@ def tile_list_flake_overlap_features_kernel(
                 if phase == 0:
                     weave(nc.vector.tensor_copy, z_round[c][b][:], z_rows[c, b][:])
                 else:
-                    second_stage(c, b)
-                    if b == 1:
+                    quantize_z(c, b)
+                    if c > 0:
+                        second_stage(c, b)
+                    if c > 0 and b == 1:
                         finish(c)
 
         uppers = [pick_upper(*steps[0])]
         for n, (c, r) in enumerate(steps):
             if n + 1 < len(steps):
                 uppers.append(pick_upper(*steps[n + 1]))
+            if c == 1 and r % PACK == 0:
+                quantize_wd(r // PACK)
+                second_stage(0, r // PACK)
+                if r == PACK:
+                    finish(0)
             pick_lower(c, r, uppers[n])
             if n >= 1:
                 after_pick(n - 1, 0)

@@ -20,8 +20,10 @@ BANK = 512
 FLOPS = 2 * K * H * S + 2 * 2 * H * N * NP
 
 CHUNKS = ((0, 256), (256, 128), (384, 128))
-WIDEST = 256
-PLANE_COLS = S + H + N
+PICKS = ((0, 384), (384, 128))
+WIDEST = 384
+EARLY_COLS = S + 512
+LATE_COLS = 512 + N
 
 
 def tile_list_flake_overlap_features_kernel(
@@ -48,13 +50,15 @@ def tile_list_flake_overlap_features_kernel(
         tab_word_rows = [held([P, T], U16, f"tab_word_rows{a}") for a in range(2)]
         weight_scale_rows = held([P, H + N], U8, "weight_scale_rows")
         gain_sb = held([P, 2, PACK], F32, "gain_sb")
-        planes = [held([P, PLANE_COLS], U8, f"planes{a}") for a in range(2)]
+        planes = [held([P, EARLY_COLS], U8, f"planes{a}") for a in range(2)]
+        late_plane1 = held([P, LATE_COLS], U8, "late_plane1")
 
         nc.vector.memset(tab_scale_rows[32:64, :].bitcast(I32), 0)
         nc.gpsimd.memset(tab_scale_rows[64:128, :].bitcast(I32), 0)
         nc.vector.memset(weight_scale_rows[32:64, :].bitcast(I32), 0)
         nc.gpsimd.memset(weight_scale_rows[64:128, :].bitcast(I32), 0)
         nc.gpsimd.memset(planes[1][:].bitcast(I32), 0)
+        nc.gpsimd.memset(late_plane1[:].bitcast(I32), 0)
 
         def load_w1(b):
             raw = held([P, 2, 512], U32, f"w1_raw{b}", "w1_raw")
@@ -90,20 +94,23 @@ def tile_list_flake_overlap_features_kernel(
             in_=gain_sb[:].rearrange("p b i -> p (b i)").unsqueeze(2).to_broadcast([P, 8, WIDEST]),
         )
 
+        def spread_planes(pair):
+            for a in (1, 0):
+                for q in range(1 - a, 4):
+                    row = 16 * a + 4 * q
+                    nc.sync.dma_start(
+                        out=pair[a][32 * q : 32 * q + 4, :].bitcast(I32),
+                        in_=pair[0][row : row + 4, :].bitcast(I32),
+                    )
+
         picked_scales = held([P, S], U8, "picked_scales")
-        nc.vector.tensor_copy(out=picked_scales[:], in_=tab_scale_rows[:].indirect(offs_sb[:]))
-        nc.gpsimd.tensor_copy(
-            out=planes[0][:, S:PLANE_COLS].rearrange("p (g i q) -> p g i q", i=PACK, q=P),
-            in_=weight_scale_rows[:].rearrange("p (g q i) -> p g i q", i=PACK, q=P),
+        nc.vector.tensor_copy(
+            out=planes[0][:, S:EARLY_COLS].rearrange("p (i q) -> p i q", i=PACK),
+            in_=weight_scale_rows[:, 0:512].rearrange("p (q i) -> p i q", i=PACK),
         )
+        nc.vector.tensor_copy(out=picked_scales[:], in_=tab_scale_rows[:].indirect(offs_sb[:]))
         nc.vector.tensor_copy(out=planes[0][:, 0:S].bitcast(I32), in_=picked_scales[:].bitcast(I32))
-        for a in range(2):
-            for q in range(1 - a, 4):
-                row = 16 * a + 4 * q
-                nc.sync.dma_start(
-                    out=planes[a][32 * q : 32 * q + 4, :].bitcast(I32),
-                    in_=planes[0][row : row + 4, :].bitcast(I32),
-                )
+        spread_planes(planes)
         v_words = [[held([P, BANK], U16, f"v_words{a}{half}") for half in range(2)] for a in range(2)]
         wd_raw = []
         for a in range(2):
@@ -112,61 +119,69 @@ def tile_list_flake_overlap_features_kernel(
                     out=v_words[a][half][:],
                     in_=tab_word_rows[a][:].indirect(offs_sb[:, 32 * half : 32 * (half + 1)]),
                 )
+        late_planes = [held([P, LATE_COLS], U8, "late_plane0", "tab_word_rows1"), late_plane1]
+        nc.vector.tensor_copy(
+            out=late_planes[0][:].rearrange("p (g i q) -> p g i q", i=PACK, q=P),
+            in_=weight_scale_rows[:, 512 : H + N].rearrange("p (g q i) -> p g i q", i=PACK, q=P),
+        )
+        spread_planes(late_planes)
 
-        w1_codes = [[None, None], [None, None]]
+        w1_codes = {}
 
-        def deal_w1(b, raw):
+        def deal_w1(b, pair, raw):
             for a in range(2):
-                w1_codes[a][b] = held([P, PACK, P], U32, f"w1_codes{a}{b}", f"w1_codes{a}")
+                w1_codes[a, b, pair] = held([P, 2, P], U32, f"w1_codes{a}{b}{pair}", f"w1_codes{a}{pair}")
                 nc.scalar.copy(
-                    out=w1_codes[a][b][:].rearrange("p i q -> p q i"),
-                    in_=raw[:, a, :].rearrange("p (q i) -> p q i", i=PACK),
+                    out=w1_codes[a, b, pair][:].rearrange("p i q -> p q i"),
+                    in_=raw[:, a, :].rearrange("p (q i) -> p q i", i=PACK)[:, :, 2 * pair : 2 * pair + 2],
                 )
 
         h_rows = [held([P, S], F32, f"h_rows{r}") for r in range(8)]
 
-        def first_pass(r, half, a):
+        def first_pass(r, half, a, bank):
             b, i = divmod(r, PACK)
             cols = slice(BANK * half, BANK * (half + 1))
             nc.tensor.matmul_mx(
-                out=banks[2 * i + half][:],
-                lhsT=w1_codes[a][b][:, i, :].bitcast(FP8X4),
-                lhsT_scale=planes[a][:, S + P * r : S + P * (r + 1)],
+                out=bank[:],
+                lhsT=w1_codes[a, b, i // 2][:, i % 2, :].bitcast(FP8X4),
+                lhsT_scale=late_planes[a][:, P * i : P * (i + 1)] if b else planes[a][:, S + P * i : S + P * (i + 1)],
                 rhs=v_words[a][half][:].bitcast(FP4X4),
                 rhs_scale=planes[a][:, cols],
                 start=(a == 0),
                 stop=(a == 1),
             )
 
-        def sigmoid(r, half):
+        def sigmoid(r, half, bank):
             nc.scalar.activation(
-                out=h_rows[r][:, BANK * half : BANK * (half + 1)], in_=banks[2 * (r % PACK) + half][:], func=ACT.Sigmoid
+                out=h_rows[r][:, BANK * half : BANK * (half + 1)], in_=bank[:], func=ACT.Sigmoid
             )
 
-        deal_w1(0, w1_raw)
+        deal_w1(0, 0, w1_raw)
+        deal_w1(0, 1, w1_raw)
+        w1_raw = load_w1(1)
         for b in range(2):
-            if b == 1:
-                w1_raw = load_w1(1)
-            raw = held([P, PACK, N], F32, f"wd_raw{b}", ("picked_scales", "tab_word_rows1")[b])
+            raw = held([P, PACK, N], F32, f"wd_raw{b}", ("tab_word_rows0", "weight_scale_rows")[b])
             nc.sync.dma_start(out=raw[:], in_=wd[512 * b : 512 * (b + 1), :].rearrange("(p i) n -> p i n", i=PACK))
             wd_raw.append(raw)
         for r in range(2 * PACK):
-            for half in range(2):
-                first_pass(r, half, 0)
-                first_pass(r, half, 1)
-                sigmoid(r, half)
-            if r == PACK - 1:
-                deal_w1(1, w1_raw)
+            for step in range(2):
+                half = (r + step) % 2
+                bank = banks[(2 * r + step) % 3]
+                first_pass(r, half, 0, bank)
+                first_pass(r, half, 1, bank)
+                sigmoid(r, half, bank)
+            if r in (1, 3):
+                deal_w1(1, r // 2, w1_raw)
 
         wn_raw = held([P, 2, N], U16, "wn_raw", "w1_raw")
         nc.sync.dma_start(out=wn_raw[:].bitcast(I32), in_=wn_words.rearrange("a p c -> p a c").bitcast(I32))
-        wn_codes = held([P, 2, PACK, P], U16, "wn_codes")
+        wn_codes = held([P, 2, PACK, P], U16, "wn_codes", "v_words11")
         wd_codes = [held([P, N], U32, f"wd_codes{b}") for b in range(2)]
         wd_planes = [held([P, N], U8, f"wd_planes{b}") for b in range(2)]
         wd_round = [None, None]
 
         def round_wd(b):
-            wd_round[b] = held([P, PACK, P, PACK], BF16, f"wd_round{b}", ("w1_codes0", "w1_codes1")[b])
+            wd_round[b] = held([P, PACK, P, PACK], BF16, f"wd_round{b}", f"w1_codes{b}1")
             dst = wd_round[b][:].rearrange("p t q i -> p q i t")
             src = wd_raw[b][:].rearrange("p i (q t) -> p q i t", t=PACK)
             nc.scalar.copy(out=dst, in_=src)
@@ -185,17 +200,21 @@ def tile_list_flake_overlap_features_kernel(
             )
 
         z_rows = {}
-        z_tags = {(1, 0): "w1_codes0", (1, 1): "w1_codes1"}
-        z_round = [[held([P, w, PACK], BF16, f"z_round{c}{b}") for b in range(2)] for c, (j0, w) in enumerate(CHUNKS)]
-        z_codes = [[held([P, w], U32, f"z_codes{c}{b}") for b in range(2)] for c, (j0, w) in enumerate(CHUNKS)]
-        z_planes = [[held([P, w], U8, f"z_planes{c}{b}") for b in range(2)] for c, (j0, w) in enumerate(CHUNKS)]
+        z_tags = {(1, 0): "w1_codes11"}
+        z_round = [[held([P, w, PACK], BF16, f"z_round{c}{b}") for b in range(2)] for c, (j0, w) in enumerate(PICKS)]
+        z_codes = [[held([P, w], U32, f"z_codes{c}{b}") for b in range(2)] for c, (j0, w) in enumerate(PICKS)]
+        z_planes = [[held([P, w], U8, f"z_planes{c}{b}") for b in range(2)] for c, (j0, w) in enumerate(PICKS)]
         y_planes = held([P, NP], U8, "y_planes")
-        low_banks = (banks[4:6], banks[0:1], banks[2:3])
-        top_banks = (banks[6:8], banks[1:2], banks[3:4])
+        low_banks = (banks[4:6], banks[3:4], banks[1:2])
+        top_banks = (banks[6:8], banks[0:1], banks[2:3])
 
         def pick_upper(c, r):
-            j0, w = CHUNKS[c]
-            upper = ring.tile([P, WIDEST], F32, name="upper", align_bytes=64)
+            j0, w = PICKS[c]
+            if (c, r) == (0, 7):
+                quantize_wd(0)
+                upper = held([P, WIDEST], F32, "upper_last", "w1_codes01")
+            else:
+                upper = ring.tile([P, WIDEST], F32, name="upper", align_bytes=64)
             nc.vector.tensor_tensor(
                 out=upper[:, 0:w],
                 in0=h_rows[r][:].indirect(pos1_sb[:, j0 // 16 : (j0 + w) // 16]),
@@ -205,7 +224,7 @@ def tile_list_flake_overlap_features_kernel(
             return upper
 
         def pick_lower(c, r, upper):
-            j0, w = CHUNKS[c]
+            j0, w = PICKS[c]
             b, i = divmod(r, PACK)
             if i == 0:
                 z_rows[c, b] = held([P, PACK, w], F32, f"z_rows{c}{b}", z_tags.get((c, b)))
@@ -230,13 +249,15 @@ def tile_list_flake_overlap_features_kernel(
         def second_stage(c, b):
             j0, w = CHUNKS[c]
             per_bank = BANK // w
+            g = c // 2
+            cols = slice(j0 - PICKS[g][0], j0 - PICKS[g][0] + w)
             for t in range(PACK):
                 nc.tensor.matmul_mx(
                     out=sum_columns(low_banks[c], w, t),
                     lhsT=wd_codes[b][:, P * t : P * (t + 1)].bitcast(FP8X4),
                     lhsT_scale=wd_planes[b][:, P * t : P * (t + 1)],
-                    rhs=z_codes[c][b][:].bitcast(FP8X4),
-                    rhs_scale=z_planes[c][b][:],
+                    rhs=z_codes[g][b][:, cols].bitcast(FP8X4),
+                    rhs_scale=z_planes[g][b][:, cols],
                     start=(b == 0 and t % per_bank == 0),
                     stop=(b == 1 and t % per_bank == per_bank - 1),
                 )
@@ -244,9 +265,9 @@ def tile_list_flake_overlap_features_kernel(
                 nc.tensor.matmul_mx(
                     out=sum_columns(top_banks[c], w, t),
                     lhsT=wn_codes[:, b, t, :].bitcast(FP4X4),
-                    lhsT_scale=planes[b][:, S + H + P * t : S + H + P * (t + 1)],
-                    rhs=z_codes[c][b][:].bitcast(FP8X4),
-                    rhs_scale=z_planes[c][b][:],
+                    lhsT_scale=late_planes[b][:, 512 + P * t : 512 + P * (t + 1)],
+                    rhs=z_codes[g][b][:, cols].bitcast(FP8X4),
+                    rhs_scale=z_planes[g][b][:, cols],
                     start=(b == 0 and t % per_bank == 0),
                     stop=(b == 1 and t % per_bank == per_bank - 1),
                 )
@@ -292,7 +313,7 @@ def tile_list_flake_overlap_features_kernel(
             for g, members in enumerate(groups):
                 width = parts[members[0]][4]
                 y_round.append(held([P, width, PACK], BF16, f"y_round{c}{g}"))
-                weave(nc.vector.tensor_copy if last else nc.scalar.copy, y_round[g][:], y_rows[g][:])
+                weave(nc.vector.tensor_copy, y_round[g][:], y_rows[g][:])
             for g, members in enumerate(groups):
                 width = parts[members[0]][4]
                 first = j0 + parts[members[0]][3]
@@ -309,8 +330,10 @@ def tile_list_flake_overlap_features_kernel(
 
         round_wd(0)
         round_wd(1)
+        warm_root = held([P, 1], F32, "warm_root")
         nc.scalar.copy(out=wn_codes[:], in_=wn_raw[:].rearrange("p b (q t) -> p b t q", t=PACK))
-        steps = [(c, r) for c in range(len(CHUNKS)) for r in range(8)]
+        nc.scalar.activation(out=warm_root[:], in_=wd_round[1][:, 0, 0, 0:1], func=ACT.Abs_reciprocal_sqrt, bias=1.0, scale=0.0)
+        steps = [(c, r) for c in range(len(PICKS)) for r in range(8)]
 
         def after_pick(n, phase):
             c, r = steps[n]
@@ -320,20 +343,22 @@ def tile_list_flake_overlap_features_kernel(
                     weave(nc.vector.tensor_copy, z_round[c][b][:], z_rows[c, b][:])
                 else:
                     quantize_z(c, b)
-                    if c > 0:
-                        second_stage(c, b)
-                    if c > 0 and b == 1:
-                        finish(c)
+                    if c == 0 and b == 1:
+                        for chunk in range(2):
+                            second_stage(chunk, 0)
+                            second_stage(chunk, 1)
+                            finish(chunk)
+                    if c == 1:
+                        second_stage(2, b)
+                    if c == 1 and b == 1:
+                        finish(2)
 
         uppers = [pick_upper(*steps[0])]
         for n, (c, r) in enumerate(steps):
             if n + 1 < len(steps):
                 uppers.append(pick_upper(*steps[n + 1]))
-            if c == 1 and r % PACK == 0:
-                quantize_wd(r // PACK)
-                second_stage(0, r // PACK)
-                if r == PACK:
-                    finish(0)
+            if c == 1 and r == 0:
+                quantize_wd(1)
             pick_lower(c, r, uppers[n])
             if n >= 1:
                 after_pick(n - 1, 0)

@@ -13,17 +13,25 @@ FP4X4 = mybir.dt.float4_e2m1fn_x4
 ACT = mybir.ActivationFunctionType
 MULT = mybir.AluOpType.mult
 
-K, T, S, NP, H, N = 1024, 4096, 1024, 512, 1024, 512
+K, T, S, PAIRS, H, N = 1024, 4096, 1024, 512, 1024, 512
+FLOPS = 2 * K * H * S + 2 * 2 * H * N * PAIRS
+
 P = 128
 PACK = 4
+PASS = P * PACK
 BANK = 512
-FLOPS = 2 * K * H * S + 2 * 2 * H * N * NP
+ROW_TILES = H // P
+PER_COLUMN = 16
+STAGE1_BANKS = 3
+UPPER_BUFS = 3
 
-CHUNKS = ((0, 256), (256, 128), (384, 128))
-PICKS = ((0, 384), (384, 128))
+ROUNDS = ((0, 384), (384, 128))
 WIDEST = 384
-EARLY_COLS = S + 512
-LATE_COLS = 512 + N
+GATHERS_PER_PICK = (2, 1)
+CHUNKS = ((0, 256), (256, 128), (384, 128))
+ROUND_OF_CHUNK = (0, 0, 1)
+EARLY_COLS = S + PASS
+LATE_COLS = PASS + N
 
 
 def tile_list_flake_overlap_features_kernel(
@@ -34,7 +42,7 @@ def tile_list_flake_overlap_features_kernel(
     with ExitStack() as ctx:
         lists = ctx.enter_context(tc.tile_pool(name="lists", bufs=1))
         keep = ctx.enter_context(tc.tile_pool(name="keep", bufs=1))
-        ring = ctx.enter_context(tc.tile_pool(name="ring", bufs=3))
+        ring = ctx.enter_context(tc.tile_pool(name="ring", bufs=UPPER_BUFS))
         psum = ctx.enter_context(tc.psum_pool(name="psum", bufs=1))
 
         def held(shape, dtype, name, tag=None):
@@ -42,29 +50,30 @@ def tile_list_flake_overlap_features_kernel(
 
         banks = [psum.tile([P, BANK], F32, name=f"bank{i}") for i in range(8)]
 
-        offs_sb = lists.tile([P, S // 16], U16, name="offs_sb")
-        pos1_sb = lists.tile([P, NP // 16], U16, name="pos1_sb")
-        pos2_sb = lists.tile([P, NP // 16], U16, name="pos2_sb")
+        offs_sb = lists.tile([P, S // PER_COLUMN], U16, name="offs_sb")
+        pos1_sb = lists.tile([P, PAIRS // PER_COLUMN], U16, name="pos1_sb")
+        pos2_sb = lists.tile([P, PAIRS // PER_COLUMN], U16, name="pos2_sb")
 
         tab_scale_rows = held([P, T], U8, "tab_scale_rows")
         tab_word_rows = [held([P, T], U16, f"tab_word_rows{a}") for a in range(2)]
         weight_scale_rows = held([P, H + N], U8, "weight_scale_rows")
         gain_sb = held([P, 2, PACK], F32, "gain_sb")
-        planes = [held([P, EARLY_COLS], U8, f"planes{a}") for a in range(2)]
+        early_planes = [held([P, EARLY_COLS], U8, f"early_plane{a}") for a in range(2)]
         late_plane1 = held([P, LATE_COLS], U8, "late_plane1")
 
         nc.vector.memset(tab_scale_rows[32:64, :].bitcast(I32), 0)
         nc.gpsimd.memset(tab_scale_rows[64:128, :].bitcast(I32), 0)
         nc.vector.memset(weight_scale_rows[32:64, :].bitcast(I32), 0)
         nc.gpsimd.memset(weight_scale_rows[64:128, :].bitcast(I32), 0)
-        nc.gpsimd.memset(planes[1][:].bitcast(I32), 0)
+        nc.gpsimd.memset(early_planes[1][:].bitcast(I32), 0)
         nc.gpsimd.memset(late_plane1[:].bitcast(I32), 0)
 
         def load_w1(b):
-            raw = held([P, 2, 512], U32, f"w1_raw{b}", "w1_raw")
+            raw = held([P, 2, PASS], U32, f"w1_raw{b}", "w1_raw")
+            word_bytes = slice(PACK * PASS * b, PACK * PASS * (b + 1))
             nc.sync.dma_start(
                 out=raw[:].bitcast(I32),
-                in_=w1_words.rearrange("a p c i -> p a (c i)")[:, :, 2048 * b : 2048 * (b + 1)].bitcast(I32),
+                in_=w1_words.rearrange("a p c i -> p a (c i)")[:, :, word_bytes].bitcast(I32),
             )
             return raw
 
@@ -86,290 +95,279 @@ def tile_list_flake_overlap_features_kernel(
         nc.sync.dma_start(out=pos2_sb[:], in_=pos2)
         nc.sync.dma_start(out=tab_word_rows[1][:].bitcast(I32), in_=tab_words[1].bitcast(I32))
 
-        warm = held([P, 1], F32, "warm")
-        nc.scalar.activation(out=warm[:], in_=gain_sb[:, 0, 0:1], func=ACT.Sigmoid)
-        gain_wide = held([P, 8, WIDEST], F32, "gain_wide")
+        warm_sigmoid = held([P, 1], F32, "warm_sigmoid")
+        nc.scalar.activation(out=warm_sigmoid[:], in_=gain_sb[:, 0, 0:1], func=ACT.Sigmoid)
+        gain_wide = held([P, ROW_TILES, WIDEST], F32, "gain_wide")
         nc.scalar.copy(
             out=gain_wide[:],
-            in_=gain_sb[:].rearrange("p b i -> p (b i)").unsqueeze(2).to_broadcast([P, 8, WIDEST]),
+            in_=gain_sb[:].rearrange("p b i -> p (b i)").unsqueeze(2).to_broadcast([P, ROW_TILES, WIDEST]),
         )
 
-        def spread_planes(pair):
+        def spread_planes(planes):
             for a in (1, 0):
-                for q in range(1 - a, 4):
-                    row = 16 * a + 4 * q
+                for quadrant in range(1 - a, 4):
+                    row = 16 * a + 4 * quadrant
                     nc.sync.dma_start(
-                        out=pair[a][32 * q : 32 * q + 4, :].bitcast(I32),
-                        in_=pair[0][row : row + 4, :].bitcast(I32),
+                        out=planes[a][32 * quadrant : 32 * quadrant + 4, :].bitcast(I32),
+                        in_=planes[0][row : row + 4, :].bitcast(I32),
                     )
 
         picked_scales = held([P, S], U8, "picked_scales")
         nc.vector.tensor_copy(
-            out=planes[0][:, S:EARLY_COLS].rearrange("p (i q) -> p i q", i=PACK),
-            in_=weight_scale_rows[:, 0:512].rearrange("p (q i) -> p i q", i=PACK),
+            out=early_planes[0][:, S:EARLY_COLS].rearrange("p (i q) -> p i q", i=PACK),
+            in_=weight_scale_rows[:, 0:PASS].rearrange("p (q i) -> p i q", i=PACK),
         )
         nc.vector.tensor_copy(out=picked_scales[:], in_=tab_scale_rows[:].indirect(offs_sb[:]))
-        nc.vector.tensor_copy(out=planes[0][:, 0:S].bitcast(I32), in_=picked_scales[:].bitcast(I32))
-        spread_planes(planes)
+        nc.vector.tensor_copy(out=early_planes[0][:, 0:S].bitcast(I32), in_=picked_scales[:].bitcast(I32))
+        spread_planes(early_planes)
         v_words = [[held([P, BANK], U16, f"v_words{a}{half}") for half in range(2)] for a in range(2)]
-        wd_raw = []
         for a in range(2):
             for half in range(2):
-                nc.vector.tensor_copy(
-                    out=v_words[a][half][:],
-                    in_=tab_word_rows[a][:].indirect(offs_sb[:, 32 * half : 32 * (half + 1)]),
-                )
+                entries = slice(BANK // PER_COLUMN * half, BANK // PER_COLUMN * (half + 1))
+                nc.vector.tensor_copy(out=v_words[a][half][:], in_=tab_word_rows[a][:].indirect(offs_sb[:, entries]))
         late_planes = [held([P, LATE_COLS], U8, "late_plane0", "tab_word_rows1"), late_plane1]
         nc.vector.tensor_copy(
             out=late_planes[0][:].rearrange("p (g i q) -> p g i q", i=PACK, q=P),
-            in_=weight_scale_rows[:, 512 : H + N].rearrange("p (g q i) -> p g i q", i=PACK, q=P),
+            in_=weight_scale_rows[:, PASS : H + N].rearrange("p (g q i) -> p g i q", i=PACK, q=P),
         )
         spread_planes(late_planes)
 
         w1_codes = {}
 
-        def deal_w1(b, pair, raw):
+        def deal_w1(b, two, raw):
             for a in range(2):
-                w1_codes[a, b, pair] = held([P, 2, P], U32, f"w1_codes{a}{b}{pair}", f"w1_codes{a}{pair}")
+                w1_codes[a, b, two] = held([P, 2, P], U32, f"w1_codes{a}{b}{two}", f"w1_codes{a}{two}")
                 nc.scalar.copy(
-                    out=w1_codes[a, b, pair][:].rearrange("p i q -> p q i"),
-                    in_=raw[:, a, :].rearrange("p (q i) -> p q i", i=PACK)[:, :, 2 * pair : 2 * pair + 2],
+                    out=w1_codes[a, b, two][:].rearrange("p i q -> p q i"),
+                    in_=raw[:, a, :].rearrange("p (q i) -> p q i", i=PACK)[:, :, 2 * two : 2 * two + 2],
                 )
 
-        h_rows = [held([P, S], F32, f"h_rows{r}") for r in range(8)]
+        h_rows = [held([P, S], F32, f"h_rows{r}") for r in range(ROW_TILES)]
 
-        def first_pass(r, half, a, bank):
+        def first_stage(r, half, bank):
             b, i = divmod(r, PACK)
             cols = slice(BANK * half, BANK * (half + 1))
-            nc.tensor.matmul_mx(
-                out=bank[:],
-                lhsT=w1_codes[a, b, i // 2][:, i % 2, :].bitcast(FP8X4),
-                lhsT_scale=late_planes[a][:, P * i : P * (i + 1)] if b else planes[a][:, S + P * i : S + P * (i + 1)],
-                rhs=v_words[a][half][:].bitcast(FP4X4),
-                rhs_scale=planes[a][:, cols],
-                start=(a == 0),
-                stop=(a == 1),
-            )
-
-        def sigmoid(r, half, bank):
-            nc.scalar.activation(
-                out=h_rows[r][:, BANK * half : BANK * (half + 1)], in_=bank[:], func=ACT.Sigmoid
-            )
+            for a in range(2):
+                w1_plane = late_planes[a][:, 0:PASS] if b else early_planes[a][:, S:EARLY_COLS]
+                nc.tensor.matmul_mx(
+                    out=bank[:],
+                    lhsT=w1_codes[a, b, i // 2][:, i % 2, :].bitcast(FP8X4),
+                    lhsT_scale=w1_plane[:, P * i : P * (i + 1)],
+                    rhs=v_words[a][half][:].bitcast(FP4X4),
+                    rhs_scale=early_planes[a][:, cols],
+                    start=(a == 0),
+                    stop=(a == 1),
+                )
+            nc.scalar.activation(out=h_rows[r][:, cols], in_=bank[:], func=ACT.Sigmoid)
 
         deal_w1(0, 0, w1_raw)
         deal_w1(0, 1, w1_raw)
         w1_raw = load_w1(1)
-        for b in range(2):
-            raw = held([P, PACK, N], F32, f"wd_raw{b}", ("tab_word_rows0", "weight_scale_rows")[b])
-            nc.sync.dma_start(out=raw[:], in_=wd[512 * b : 512 * (b + 1), :].rearrange("(p i) n -> p i n", i=PACK))
+        wd_raw = []
+        for b, tag in enumerate(("tab_word_rows0", "weight_scale_rows")):
+            raw = held([P, PACK, N], F32, f"wd_raw{b}", tag)
+            nc.sync.dma_start(out=raw[:], in_=wd[PASS * b : PASS * (b + 1), :].rearrange("(p i) n -> p i n", i=PACK))
             wd_raw.append(raw)
-        for r in range(2 * PACK):
+        for r in range(ROW_TILES):
             for step in range(2):
-                half = (r + step) % 2
-                bank = banks[(2 * r + step) % 3]
-                first_pass(r, half, 0, bank)
-                first_pass(r, half, 1, bank)
-                sigmoid(r, half, bank)
-            if r in (1, 3):
+                first_stage(r, (r + step) % 2, banks[(2 * r + step) % STAGE1_BANKS])
+            if r < PACK and r % 2 == 1:
                 deal_w1(1, r // 2, w1_raw)
 
         wn_raw = held([P, 2, N], U16, "wn_raw", "w1_raw")
-        nc.sync.dma_start(out=wn_raw[:].bitcast(I32), in_=wn_words.rearrange("a p c -> p a c").bitcast(I32))
+        nc.sync.dma_start(out=wn_raw[:].bitcast(I32), in_=wn_words.rearrange("b p c -> p b c").bitcast(I32))
         wn_codes = held([P, 2, PACK, P], U16, "wn_codes", "v_words11")
         wd_codes = [held([P, N], U32, f"wd_codes{b}") for b in range(2)]
         wd_planes = [held([P, N], U8, f"wd_planes{b}") for b in range(2)]
-        wd_round = [None, None]
+        wd_round = []
+        for b in range(2):
+            wd_round.append(held([P, PACK, P, PACK], BF16, f"wd_round{b}", f"w1_codes{b}1"))
+            nc.scalar.copy(
+                out=wd_round[b][:].rearrange("p t q i -> p q i t"),
+                in_=wd_raw[b][:].rearrange("p i (q t) -> p q i t", t=PACK),
+            )
+        nc.scalar.copy(out=wn_codes[:], in_=wn_raw[:].rearrange("p b (q t) -> p b t q", t=PACK))
+        warm_root = held([P, 1], F32, "warm_root")
+        nc.scalar.activation(
+            out=warm_root[:], in_=wd_round[1][:, 0, 0, 0:1], func=ACT.Abs_reciprocal_sqrt, bias=1.0, scale=0.0
+        )
 
-        def round_wd(b):
-            wd_round[b] = held([P, PACK, P, PACK], BF16, f"wd_round{b}", f"w1_codes{b}1")
-            dst = wd_round[b][:].rearrange("p t q i -> p q i t")
-            src = wd_raw[b][:].rearrange("p i (q t) -> p q i t", t=PACK)
-            nc.scalar.copy(out=dst, in_=src)
+        def quantize(codes, plane, rounded):
+            nc.vector.quantize_mx(out=codes.bitcast(FP8X4), scales=plane, in_=rounded)
 
         def quantize_wd(b):
-            nc.vector.quantize_mx(
-                out=wd_codes[b][:].bitcast(FP8X4),
-                scales=wd_planes[b][:],
-                in_=wd_round[b][:].rearrange("p t q i -> p (t q i)"),
-            )
+            quantize(wd_codes[b][:], wd_planes[b][:], wd_round[b][:].rearrange("p t q i -> p (t q i)"))
 
-        def weave(engine_copy, dst, src):
-            engine_copy(
-                out=dst.rearrange("p (c n) t -> p c t n", n=4),
-                in_=src.rearrange("p t (c n) -> p c t n", n=4),
+        def weave(rounded, rows):
+            nc.vector.tensor_copy(
+                out=rounded.rearrange("p (c n) t -> p c t n", n=4),
+                in_=rows.rearrange("p t (c n) -> p c t n", n=4),
             )
 
         z_rows = {}
-        z_tags = {(1, 0): "w1_codes11"}
-        z_round = [[held([P, w, PACK], BF16, f"z_round{c}{b}") for b in range(2)] for c, (j0, w) in enumerate(PICKS)]
-        z_codes = [[held([P, w], U32, f"z_codes{c}{b}") for b in range(2)] for c, (j0, w) in enumerate(PICKS)]
-        z_planes = [[held([P, w], U8, f"z_planes{c}{b}") for b in range(2)] for c, (j0, w) in enumerate(PICKS)]
-        y_planes = held([P, NP], U8, "y_planes")
+        z_round = [[held([P, w, PACK], BF16, f"z_round{g}{b}") for b in range(2)] for g, (j0, w) in enumerate(ROUNDS)]
+        z_codes = [[held([P, w], U32, f"z_codes{g}{b}") for b in range(2)] for g, (j0, w) in enumerate(ROUNDS)]
+        z_planes = [[held([P, w], U8, f"z_planes{g}{b}") for b in range(2)] for g, (j0, w) in enumerate(ROUNDS)]
+        y_plane = held([P, PAIRS], U8, "y_plane")
         low_banks = (banks[4:6], banks[3:4], banks[1:2])
         top_banks = (banks[6:8], banks[0:1], banks[2:3])
 
-        def pick_upper(c, r):
-            j0, w = PICKS[c]
-            if (c, r) == (0, 7):
+        def gathers_of(g):
+            j0, w = ROUNDS[g]
+            width = w // GATHERS_PER_PICK[g]
+            return [
+                (slice(c0, c0 + width), slice((j0 + c0) // PER_COLUMN, (j0 + c0 + width) // PER_COLUMN))
+                for c0 in range(0, w, width)
+            ]
+
+        def pick_upper(g, r):
+            if (g, r) == (0, ROW_TILES - 1):
                 quantize_wd(0)
                 upper = held([P, WIDEST], F32, "upper_last", "w1_codes01")
             else:
                 upper = ring.tile([P, WIDEST], F32, name="upper", align_bytes=64)
-            nc.vector.tensor_tensor(
-                out=upper[:, 0:w],
-                in0=h_rows[r][:].indirect(pos1_sb[:, j0 // 16 : (j0 + w) // 16]),
-                in1=gain_wide[:, r, 0:w],
-                op=MULT,
-            )
+            for cols, entries in gathers_of(g):
+                nc.vector.tensor_tensor(
+                    out=upper[:, cols],
+                    in0=h_rows[r][:].indirect(pos1_sb[:, entries]),
+                    in1=gain_wide[:, r, cols],
+                    op=MULT,
+                )
             return upper
 
-        def pick_lower(c, r, upper):
-            j0, w = PICKS[c]
+        def pick_lower(g, r, upper):
             b, i = divmod(r, PACK)
+            if (g, r) == (1, 0):
+                quantize_wd(1)
             if i == 0:
-                z_rows[c, b] = held([P, PACK, w], F32, f"z_rows{c}{b}", z_tags.get((c, b)))
-            nc.vector.tensor_tensor(
-                out=z_rows[c, b][:, i, :],
-                in0=h_rows[r][:].indirect(pos2_sb[:, j0 // 16 : (j0 + w) // 16]),
-                in1=upper[:, 0:w],
-                op=MULT,
-            )
-
-        def sum_columns(bank_list, w, t):
-            per_bank = BANK // w
-            return bank_list[t // per_bank][:, (t % per_bank) * w : (t % per_bank + 1) * w]
-
-        def quantize_z(c, b):
-            nc.vector.quantize_mx(
-                out=z_codes[c][b][:].bitcast(FP8X4),
-                scales=z_planes[c][b][:],
-                in_=z_round[c][b][:].rearrange("p j t -> p (j t)"),
-            )
+                tag = "w1_codes11" if (g, r) == (1, 0) else None
+                z_rows[g, b] = held([P, PACK, ROUNDS[g][1]], F32, f"z_rows{g}{b}", tag)
+            for cols, entries in gathers_of(g):
+                nc.vector.tensor_tensor(
+                    out=z_rows[g, b][:, i, cols],
+                    in0=h_rows[r][:].indirect(pos2_sb[:, entries]),
+                    in1=upper[:, cols],
+                    op=MULT,
+                )
 
         def second_stage(c, b):
             j0, w = CHUNKS[c]
+            g = ROUND_OF_CHUNK[c]
             per_bank = BANK // w
-            g = c // 2
-            cols = slice(j0 - PICKS[g][0], j0 - PICKS[g][0] + w)
-            for t in range(PACK):
-                nc.tensor.matmul_mx(
-                    out=sum_columns(low_banks[c], w, t),
-                    lhsT=wd_codes[b][:, P * t : P * (t + 1)].bitcast(FP8X4),
-                    lhsT_scale=wd_planes[b][:, P * t : P * (t + 1)],
-                    rhs=z_codes[g][b][:, cols].bitcast(FP8X4),
-                    rhs_scale=z_planes[g][b][:, cols],
-                    start=(b == 0 and t % per_bank == 0),
-                    stop=(b == 1 and t % per_bank == per_bank - 1),
-                )
-            for t in range(PACK):
-                nc.tensor.matmul_mx(
-                    out=sum_columns(top_banks[c], w, t),
-                    lhsT=wn_codes[:, b, t, :].bitcast(FP4X4),
-                    lhsT_scale=late_planes[b][:, 512 + P * t : 512 + P * (t + 1)],
-                    rhs=z_codes[g][b][:, cols].bitcast(FP8X4),
-                    rhs_scale=z_planes[g][b][:, cols],
-                    start=(b == 0 and t % per_bank == 0),
-                    stop=(b == 1 and t % per_bank == per_bank - 1),
-                )
-
-        def finish(c):
-            j0, w = CHUNKS[c]
-            last = c == len(CHUNKS) - 1
-            per_bank = BANK // w
-            if last:
-                parts = [(0, 0, PACK, (w // 2) * u, w // 2) for u in range(2)]
-            else:
-                parts = [(k, per_bank * k, per_bank, 0, w) for k in range(len(low_banks[c]))]
-            groups = [[0], [1]] if last else [list(range(len(parts)))]
-
-            def sums(bank_list, part):
-                k, t0, nt, c0, nc_ = part
-                return bank_list[k][:].rearrange("p (t j) -> p t j", j=w)[:, :, c0 : c0 + nc_]
-
-            size = [held([P, p[2], p[4]], F32, f"size{c}{u}") for u, p in enumerate(parts)]
-            root = [held([P, p[2], p[4]], F32, f"root{c}{u}") for u, p in enumerate(parts)]
-            damp = [held([P, p[2], p[4]], F32, f"damp{c}{u}") for u, p in enumerate(parts)]
-            for u, part in enumerate(parts):
-                nc.scalar.activation(out=size[u][:], in_=sums(low_banks[c], part), func=ACT.Abs)
-            for u, part in enumerate(parts):
-                nc.scalar.activation(out=root[u][:], in_=size[u][:], func=ACT.Abs_reciprocal_sqrt, bias=1.0)
-            for u, part in enumerate(parts):
-                nc.scalar.activation(out=damp[u][:], in_=root[u][:], func=ACT.Square)
-            y_rows = []
-            for g, members in enumerate(groups):
-                width = parts[members[0]][4]
-                rows = held([P, PACK, width], F32, f"y_rows{c}{g}")
-                y_rows.append(rows)
-                for u in members:
-                    k, t0, nt, c0, nc_ = parts[u]
-                    nc.vector.tensor_tensor(
-                        out=rows[:, t0 : t0 + nt, :], in0=sums(top_banks[c], parts[u]), in1=damp[u][:], op=MULT
+            cols = slice(j0 - ROUNDS[g][0], j0 - ROUNDS[g][0] + w)
+            low_weights = [
+                (wd_codes[b][:, P * t : P * (t + 1)].bitcast(FP8X4), wd_planes[b][:, P * t : P * (t + 1)])
+                for t in range(PACK)
+            ]
+            top_weights = [
+                (wn_codes[:, b, t, :].bitcast(FP4X4), late_planes[b][:, PASS + P * t : PASS + P * (t + 1)])
+                for t in range(PACK)
+            ]
+            for sum_banks, weights in ((low_banks[c], low_weights), (top_banks[c], top_weights)):
+                for t, (codes, plane) in enumerate(weights):
+                    place = t % per_bank
+                    nc.tensor.matmul_mx(
+                        out=sum_banks[t // per_bank][:, place * w : (place + 1) * w],
+                        lhsT=codes,
+                        lhsT_scale=plane,
+                        rhs=z_codes[g][b][:, cols].bitcast(FP8X4),
+                        rhs_scale=z_planes[g][b][:, cols],
+                        start=(b == 0 and place == 0),
+                        stop=(b == 1 and place == per_bank - 1),
                     )
-                first = j0 + parts[members[0]][3]
+
+        def pieces(c):
+            w = CHUNKS[c][1]
+            if c == len(CHUNKS) - 1:
+                return [(0, 0, PACK, w // 2 * u, w // 2) for u in range(2)]
+            per_bank = BANK // w
+            return [(k, per_bank * k, per_bank, 0, w) for k in range(PACK // per_bank)]
+
+        def sums_of(sum_banks, c, piece):
+            k, slot0, slots, col0, width = piece
+            return sum_banks[k][:].rearrange("p (t j) -> p t j", j=CHUNKS[c][1])[:, :, col0 : col0 + width]
+
+        damp = {}
+
+        def damping(c):
+            size = [held([P, p[2], p[4]], F32, f"size{c}{u}") for u, p in enumerate(pieces(c))]
+            root = [held([P, p[2], p[4]], F32, f"root{c}{u}") for u, p in enumerate(pieces(c))]
+            damp[c] = [held([P, p[2], p[4]], F32, f"damp{c}{u}") for u, p in enumerate(pieces(c))]
+            for u, piece in enumerate(pieces(c)):
+                nc.scalar.activation(out=size[u][:], in_=sums_of(low_banks[c], c, piece), func=ACT.Abs)
+            for u in range(len(size)):
+                nc.scalar.activation(out=root[u][:], in_=size[u][:], func=ACT.Abs_reciprocal_sqrt, bias=1.0)
+            for u in range(len(size)):
+                nc.scalar.activation(out=damp[c][u][:], in_=root[u][:], func=ACT.Square)
+
+        def hand_out(c, tag):
+            j0 = CHUNKS[c][0]
+            spans = sorted({(p[3], p[4]) for p in pieces(c)})
+            y_rows = []
+            for col0, width in spans:
+                rows = held([P, PACK, width], F32, f"y_rows{c}_{col0}", tag)
+                y_rows.append(rows)
+                for u, piece in enumerate(pieces(c)):
+                    if piece[3] == col0:
+                        nc.vector.tensor_tensor(
+                            out=rows[:, piece[1] : piece[1] + piece[2], :],
+                            in0=sums_of(top_banks[c], c, piece),
+                            in1=damp[c][u][:],
+                            op=MULT,
+                        )
                 nc.sync.dma_start(
-                    out=out_0.rearrange("(p t) j -> p t j", t=PACK)[:, :, first : first + width], in_=rows[:]
+                    out=out_0.rearrange("(p t) j -> p t j", t=PACK)[:, :, j0 + col0 : j0 + col0 + width], in_=rows[:]
                 )
             y_round = []
-            for g, members in enumerate(groups):
-                width = parts[members[0]][4]
-                y_round.append(held([P, width, PACK], BF16, f"y_round{c}{g}"))
-                weave(nc.vector.tensor_copy, y_round[g][:], y_rows[g][:])
-            for g, members in enumerate(groups):
-                width = parts[members[0]][4]
-                first = j0 + parts[members[0]][3]
-                y_codes = held([P, width], U32, f"y_codes{c}{g}")
-                nc.vector.quantize_mx(
-                    out=y_codes[:].bitcast(FP8X4),
-                    scales=y_planes[:, first : first + width],
-                    in_=y_round[g][:].rearrange("p j t -> p (j t)"),
-                )
+            for (col0, width), rows in zip(spans, y_rows):
+                y_round.append(held([P, width, PACK], BF16, f"y_round{c}_{col0}"))
+                weave(y_round[-1][:], rows[:])
+            for (col0, width), rounded in zip(spans, y_round):
+                first = j0 + col0
+                y_codes = held([P, width], U32, f"y_codes{c}_{col0}")
+                quantize(y_codes[:], y_plane[:, first : first + width], rounded[:].rearrange("p j t -> p (j t)"))
                 nc.sync.dma_start(
-                    out=out_1[0].rearrange("p m t -> p (m t)")[:, 4 * first : 4 * (first + width)].bitcast(I32),
+                    out=out_1[0].rearrange("p m t -> p (m t)")[:, PACK * first : PACK * (first + width)].bitcast(I32),
                     in_=y_codes[:].bitcast(I32),
                 )
 
-        round_wd(0)
-        round_wd(1)
-        warm_root = held([P, 1], F32, "warm_root")
-        nc.scalar.copy(out=wn_codes[:], in_=wn_raw[:].rearrange("p b (q t) -> p b t q", t=PACK))
-        nc.scalar.activation(out=warm_root[:], in_=wd_round[1][:, 0, 0, 0:1], func=ACT.Abs_reciprocal_sqrt, bias=1.0, scale=0.0)
-        steps = [(c, r) for c in range(len(PICKS)) for r in range(8)]
+        steps = [(g, r) for g in range(len(ROUNDS)) for r in range(ROW_TILES)]
 
-        def after_pick(n, phase):
-            c, r = steps[n]
+        def weave_z(n):
+            g, r = steps[n]
+            if r % PACK == PACK - 1:
+                weave(z_round[g][r // PACK][:], z_rows[g, r // PACK][:])
+
+        def multiply_z(n):
+            g, r = steps[n]
             b = r // PACK
             if r % PACK == PACK - 1:
-                if phase == 0:
-                    weave(nc.vector.tensor_copy, z_round[c][b][:], z_rows[c, b][:])
-                else:
-                    quantize_z(c, b)
-                    if c == 0 and b == 1:
-                        for chunk in range(2):
-                            second_stage(chunk, 0)
-                            second_stage(chunk, 1)
-                            finish(chunk)
-                    if c == 1:
-                        second_stage(2, b)
-                    if c == 1 and b == 1:
-                        finish(2)
+                quantize(z_codes[g][b][:], z_planes[g][b][:], z_round[g][b][:].rearrange("p j t -> p (j t)"))
+            if r == ROW_TILES - 1:
+                for c in range(len(CHUNKS)):
+                    if ROUND_OF_CHUNK[c] == g:
+                        second_stage(c, 0)
+                        second_stage(c, 1)
+                        damping(c)
 
         uppers = [pick_upper(*steps[0])]
-        for n, (c, r) in enumerate(steps):
+        for n, (g, r) in enumerate(steps):
             if n + 1 < len(steps):
                 uppers.append(pick_upper(*steps[n + 1]))
-            if c == 1 and r == 0:
-                quantize_wd(1)
-            pick_lower(c, r, uppers[n])
+            pick_lower(g, r, uppers[n])
             if n >= 1:
-                after_pick(n - 1, 0)
+                weave_z(n - 1)
             if n >= 2:
-                after_pick(n - 2, 1)
-        after_pick(len(steps) - 1, 0)
-        after_pick(len(steps) - 1, 1)
+                multiply_z(n - 2)
+        weave_z(len(steps) - 1)
+        multiply_z(len(steps) - 1)
 
-        for q in range(4):
-            queue = nc.scalar if q % 2 else nc.sync
+        for c, tag in enumerate(("z_round11", "damp01", None)):
+            hand_out(c, tag)
+
+        for quadrant in range(4):
+            queue = nc.scalar if quadrant % 2 else nc.sync
             queue.dma_start(
-                out=out_2[0, 4 * q : 4 * q + 4, :].bitcast(I32),
-                in_=y_planes[32 * q : 32 * q + 4, :].bitcast(I32),
+                out=out_2[0, 4 * quadrant : 4 * quadrant + 4, :].bitcast(I32),
+                in_=y_plane[32 * quadrant : 32 * quadrant + 4, :].bitcast(I32),
             )

from contextlib import ExitStack

import concourse.mybir as mybir

F32 = mybir.dt.float32
BF16 = mybir.dt.bfloat16
I32 = mybir.dt.int32
U32 = mybir.dt.uint32
U16 = mybir.dt.uint16
U8 = mybir.dt.uint8
FP8X4 = mybir.dt.float8_e4m3fn_x4
FP4X4 = mybir.dt.float4_e2m1fn_x4
ACT = mybir.ActivationFunctionType
MULT = mybir.AluOpType.mult

K, T, S, PAIRS, H, N = 1024, 4096, 1024, 512, 1024, 512
FLOPS = 2 * K * H * S + 2 * 2 * H * N * PAIRS

P = 128
PACK = 4
PASS = P * PACK
BANK = 512
ROW_TILES = H // P
PER_COLUMN = 16
STAGE1_BANKS = 3
UPPER_BUFS = 3

ROUNDS = ((0, 384), (384, 128))
WIDEST = 384
GATHERS_PER_PICK = (2, 1)
CHUNKS = ((0, 256), (256, 128), (384, 128))
ROUND_OF_CHUNK = (0, 0, 1)
EARLY_COLS = S + PASS
LATE_COLS = PASS + N


def tile_list_flake_overlap_features_kernel(
    tc, tab_words, tab_scales, offs, pos1, pos2, w1_words, w1_scales, gain, wn_words, wn_scales, wd,
    out_0, out_1, out_2,
):
    nc = tc.nc
    with ExitStack() as ctx:
        lists = ctx.enter_context(tc.tile_pool(name="lists", bufs=1))
        keep = ctx.enter_context(tc.tile_pool(name="keep", bufs=1))
        ring = ctx.enter_context(tc.tile_pool(name="ring", bufs=UPPER_BUFS))
        psum = ctx.enter_context(tc.psum_pool(name="psum", bufs=1))

        def held(shape, dtype, name, tag=None):
            return keep.tile(shape, dtype, name=name, tag=tag or name, align_bytes=64)

        banks = [psum.tile([P, BANK], F32, name=f"bank{i}") for i in range(8)]

        offs_sb = lists.tile([P, S // PER_COLUMN], U16, name="offs_sb")
        pos1_sb = lists.tile([P, PAIRS // PER_COLUMN], U16, name="pos1_sb")
        pos2_sb = lists.tile([P, PAIRS // PER_COLUMN], U16, name="pos2_sb")

        tab_scale_rows = held([P, T], U8, "tab_scale_rows")
        tab_word_rows = [held([P, T], U16, f"tab_word_rows{a}") for a in range(2)]
        weight_scale_rows = held([P, H + N], U8, "weight_scale_rows")
        gain_sb = held([P, 2, PACK], F32, "gain_sb")
        early_planes = [held([P, EARLY_COLS], U8, f"early_plane{a}") for a in range(2)]
        late_plane1 = held([P, LATE_COLS], U8, "late_plane1")

        nc.vector.memset(tab_scale_rows[32:64, :].bitcast(I32), 0)
        nc.gpsimd.memset(tab_scale_rows[64:128, :].bitcast(I32), 0)
        nc.vector.memset(weight_scale_rows[32:64, :].bitcast(I32), 0)
        nc.gpsimd.memset(weight_scale_rows[64:128, :].bitcast(I32), 0)
        nc.gpsimd.memset(early_planes[1][:].bitcast(I32), 0)
        nc.gpsimd.memset(late_plane1[:].bitcast(I32), 0)

        def load_w1(b):
            raw = held([P, 2, PASS], U32, f"w1_raw{b}", "w1_raw")
            word_bytes = slice(PACK * PASS * b, PACK * PASS * (b + 1))
            nc.sync.dma_start(
                out=raw[:].bitcast(I32),
                in_=w1_words.rearrange("a p c i -> p a (c i)")[:, :, word_bytes].bitcast(I32),
            )
            return raw

        nc.sync.dma_start(out=offs_sb[:], in_=offs)
        nc.scalar.dma_start(out=gain_sb[:], in_=gain.rearrange("(b p i) -> p b i", b=2, i=PACK))
        nc.sync.dma_start(
            out=tab_scale_rows[0:32, :].bitcast(I32), in_=tab_scales.rearrange("a q t -> (a q) t").bitcast(I32)
        )
        nc.sync.dma_start(
            out=weight_scale_rows[0:32, 0:H].bitcast(I32), in_=w1_scales.rearrange("a q c -> (a q) c").bitcast(I32)
        )
        nc.sync.dma_start(
            out=weight_scale_rows[0:32, H : H + N].bitcast(I32),
            in_=wn_scales.rearrange("a q c -> (a q) c").bitcast(I32),
        )
        nc.sync.dma_start(out=tab_word_rows[0][:].bitcast(I32), in_=tab_words[0].bitcast(I32))
        w1_raw = load_w1(0)
        nc.sync.dma_start(out=pos1_sb[:], in_=pos1)
        nc.sync.dma_start(out=pos2_sb[:], in_=pos2)
        nc.sync.dma_start(out=tab_word_rows[1][:].bitcast(I32), in_=tab_words[1].bitcast(I32))

        warm_sigmoid = held([P, 1], F32, "warm_sigmoid")
        nc.scalar.activation(out=warm_sigmoid[:], in_=gain_sb[:, 0, 0:1], func=ACT.Sigmoid)
        gain_wide = held([P, ROW_TILES, WIDEST], F32, "gain_wide")
        nc.scalar.copy(
            out=gain_wide[:],
            in_=gain_sb[:].rearrange("p b i -> p (b i)").unsqueeze(2).to_broadcast([P, ROW_TILES, WIDEST]),
        )

        def spread_planes(planes):
            for a in (1, 0):
                for quadrant in range(1 - a, 4):
                    row = 16 * a + 4 * quadrant
                    nc.sync.dma_start(
                        out=planes[a][32 * quadrant : 32 * quadrant + 4, :].bitcast(I32),
                        in_=planes[0][row : row + 4, :].bitcast(I32),
                    )

        picked_scales = held([P, S], U8, "picked_scales")
        nc.vector.tensor_copy(
            out=early_planes[0][:, S:EARLY_COLS].rearrange("p (i q) -> p i q", i=PACK),
            in_=weight_scale_rows[:, 0:PASS].rearrange("p (q i) -> p i q", i=PACK),
        )
        nc.vector.tensor_copy(out=picked_scales[:], in_=tab_scale_rows[:].indirect(offs_sb[:]))
        nc.vector.tensor_copy(out=early_planes[0][:, 0:S].bitcast(I32), in_=picked_scales[:].bitcast(I32))
        spread_planes(early_planes)
        v_words = [[held([P, BANK], U16, f"v_words{a}{half}") for half in range(2)] for a in range(2)]
        for a in range(2):
            for half in range(2):
                entries = slice(BANK // PER_COLUMN * half, BANK // PER_COLUMN * (half + 1))
                nc.vector.tensor_copy(out=v_words[a][half][:], in_=tab_word_rows[a][:].indirect(offs_sb[:, entries]))
        late_planes = [held([P, LATE_COLS], U8, "late_plane0", "tab_word_rows1"), late_plane1]
        nc.vector.tensor_copy(
            out=late_planes[0][:].rearrange("p (g i q) -> p g i q", i=PACK, q=P),
            in_=weight_scale_rows[:, PASS : H + N].rearrange("p (g q i) -> p g i q", i=PACK, q=P),
        )
        spread_planes(late_planes)

        w1_codes = {}

        def deal_w1(b, two, raw):
            for a in range(2):
                w1_codes[a, b, two] = held([P, 2, P], U32, f"w1_codes{a}{b}{two}", f"w1_codes{a}{two}")
                nc.scalar.copy(
                    out=w1_codes[a, b, two][:].rearrange("p i q -> p q i"),
                    in_=raw[:, a, :].rearrange("p (q i) -> p q i", i=PACK)[:, :, 2 * two : 2 * two + 2],
                )

        h_rows = [held([P, S], F32, f"h_rows{r}") for r in range(ROW_TILES)]

        def first_stage(r, half, bank):
            b, i = divmod(r, PACK)
            cols = slice(BANK * half, BANK * (half + 1))
            for a in range(2):
                w1_plane = late_planes[a][:, 0:PASS] if b else early_planes[a][:, S:EARLY_COLS]
                nc.tensor.matmul_mx(
                    out=bank[:],
                    lhsT=w1_codes[a, b, i // 2][:, i % 2, :].bitcast(FP8X4),
                    lhsT_scale=w1_plane[:, P * i : P * (i + 1)],
                    rhs=v_words[a][half][:].bitcast(FP4X4),
                    rhs_scale=early_planes[a][:, cols],
                    start=(a == 0),
                    stop=(a == 1),
                )
            nc.scalar.activation(out=h_rows[r][:, cols], in_=bank[:], func=ACT.Sigmoid)

        deal_w1(0, 0, w1_raw)
        deal_w1(0, 1, w1_raw)
        w1_raw = load_w1(1)
        wd_raw = []
        for b, tag in enumerate(("tab_word_rows0", "weight_scale_rows")):
            raw = held([P, PACK, N], F32, f"wd_raw{b}", tag)
            nc.sync.dma_start(out=raw[:], in_=wd[PASS * b : PASS * (b + 1), :].rearrange("(p i) n -> p i n", i=PACK))
            wd_raw.append(raw)
        for r in range(ROW_TILES):
            for step in range(2):
                first_stage(r, (r + step) % 2, banks[(2 * r + step) % STAGE1_BANKS])
            if r < PACK and r % 2 == 1:
                deal_w1(1, r // 2, w1_raw)

        wn_raw = held([P, 2, N], U16, "wn_raw", "w1_raw")
        nc.sync.dma_start(out=wn_raw[:].bitcast(I32), in_=wn_words.rearrange("b p c -> p b c").bitcast(I32))
        wn_codes = held([P, 2, PACK, P], U16, "wn_codes", "v_words11")
        wd_codes = [held([P, N], U32, f"wd_codes{b}") for b in range(2)]
        wd_planes = [held([P, N], U8, f"wd_planes{b}") for b in range(2)]
        wd_round = []
        for b in range(2):
            wd_round.append(held([P, PACK, P, PACK], BF16, f"wd_round{b}", f"w1_codes{b}1"))
            nc.scalar.copy(
                out=wd_round[b][:].rearrange("p t q i -> p q i t"),
                in_=wd_raw[b][:].rearrange("p i (q t) -> p q i t", t=PACK),
            )
        nc.scalar.copy(out=wn_codes[:], in_=wn_raw[:].rearrange("p b (q t) -> p b t q", t=PACK))
        warm_root = held([P, 1], F32, "warm_root")
        nc.scalar.activation(
            out=warm_root[:], in_=wd_round[1][:, 0, 0, 0:1], func=ACT.Abs_reciprocal_sqrt, bias=1.0, scale=0.0
        )

        def quantize(codes, plane, rounded):
            nc.vector.quantize_mx(out=codes.bitcast(FP8X4), scales=plane, in_=rounded)

        def quantize_wd(b):
            quantize(wd_codes[b][:], wd_planes[b][:], wd_round[b][:].rearrange("p t q i -> p (t q i)"))

        def weave(rounded, rows):
            nc.vector.tensor_copy(
                out=rounded.rearrange("p (c n) t -> p c t n", n=4),
                in_=rows.rearrange("p t (c n) -> p c t n", n=4),
            )

        z_rows = {}
        z_round = [[held([P, w, PACK], BF16, f"z_round{g}{b}") for b in range(2)] for g, (j0, w) in enumerate(ROUNDS)]
        z_codes = [[held([P, w], U32, f"z_codes{g}{b}") for b in range(2)] for g, (j0, w) in enumerate(ROUNDS)]
        z_planes = [[held([P, w], U8, f"z_planes{g}{b}") for b in range(2)] for g, (j0, w) in enumerate(ROUNDS)]
        y_plane = held([P, PAIRS], U8, "y_plane")
        low_banks = (banks[4:6], banks[3:4], banks[1:2])
        top_banks = (banks[6:8], banks[0:1], banks[2:3])

        def gathers_of(g):
            j0, w = ROUNDS[g]
            width = w // GATHERS_PER_PICK[g]
            return [
                (slice(c0, c0 + width), slice((j0 + c0) // PER_COLUMN, (j0 + c0 + width) // PER_COLUMN))
                for c0 in range(0, w, width)
            ]

        def pick_upper(g, r):
            if (g, r) == (0, ROW_TILES - 1):
                quantize_wd(0)
                upper = held([P, WIDEST], F32, "upper_last", "w1_codes01")
            else:
                upper = ring.tile([P, WIDEST], F32, name="upper", align_bytes=64)
            for cols, entries in gathers_of(g):
                nc.vector.tensor_tensor(
                    out=upper[:, cols],
                    in0=h_rows[r][:].indirect(pos1_sb[:, entries]),
                    in1=gain_wide[:, r, cols],
                    op=MULT,
                )
            return upper

        def pick_lower(g, r, upper):
            b, i = divmod(r, PACK)
            if (g, r) == (1, 0):
                quantize_wd(1)
            if i == 0:
                tag = "w1_codes11" if (g, r) == (1, 0) else None
                z_rows[g, b] = held([P, PACK, ROUNDS[g][1]], F32, f"z_rows{g}{b}", tag)
            for cols, entries in gathers_of(g):
                nc.vector.tensor_tensor(
                    out=z_rows[g, b][:, i, cols],
                    in0=h_rows[r][:].indirect(pos2_sb[:, entries]),
                    in1=upper[:, cols],
                    op=MULT,
                )

        def second_stage(c, b):
            j0, w = CHUNKS[c]
            g = ROUND_OF_CHUNK[c]
            per_bank = BANK // w
            cols = slice(j0 - ROUNDS[g][0], j0 - ROUNDS[g][0] + w)
            low_weights = [
                (wd_codes[b][:, P * t : P * (t + 1)].bitcast(FP8X4), wd_planes[b][:, P * t : P * (t + 1)])
                for t in range(PACK)
            ]
            top_weights = [
                (wn_codes[:, b, t, :].bitcast(FP4X4), late_planes[b][:, PASS + P * t : PASS + P * (t + 1)])
                for t in range(PACK)
            ]
            for sum_banks, weights in ((low_banks[c], low_weights), (top_banks[c], top_weights)):
                for t, (codes, plane) in enumerate(weights):
                    place = t % per_bank
                    nc.tensor.matmul_mx(
                        out=sum_banks[t // per_bank][:, place * w : (place + 1) * w],
                        lhsT=codes,
                        lhsT_scale=plane,
                        rhs=z_codes[g][b][:, cols].bitcast(FP8X4),
                        rhs_scale=z_planes[g][b][:, cols],
                        start=(b == 0 and place == 0),
                        stop=(b == 1 and place == per_bank - 1),
                    )

        def pieces(c):
            w = CHUNKS[c][1]
            if c == len(CHUNKS) - 1:
                return [(0, 0, PACK, w // 2 * u, w // 2) for u in range(2)]
            per_bank = BANK // w
            return [(k, per_bank * k, per_bank, 0, w) for k in range(PACK // per_bank)]

        def sums_of(sum_banks, c, piece):
            k, slot0, slots, col0, width = piece
            return sum_banks[k][:].rearrange("p (t j) -> p t j", j=CHUNKS[c][1])[:, :, col0 : col0 + width]

        damp = {}

        def damping(c):
            size = [held([P, p[2], p[4]], F32, f"size{c}{u}") for u, p in enumerate(pieces(c))]
            root = [held([P, p[2], p[4]], F32, f"root{c}{u}") for u, p in enumerate(pieces(c))]
            damp[c] = [held([P, p[2], p[4]], F32, f"damp{c}{u}") for u, p in enumerate(pieces(c))]
            for u, piece in enumerate(pieces(c)):
                nc.scalar.activation(out=size[u][:], in_=sums_of(low_banks[c], c, piece), func=ACT.Abs)
            for u in range(len(size)):
                nc.scalar.activation(out=root[u][:], in_=size[u][:], func=ACT.Abs_reciprocal_sqrt, bias=1.0)
            for u in range(len(size)):
                nc.scalar.activation(out=damp[c][u][:], in_=root[u][:], func=ACT.Square)

        def hand_out(c, tag):
            j0 = CHUNKS[c][0]
            spans = sorted({(p[3], p[4]) for p in pieces(c)})
            y_rows = []
            for col0, width in spans:
                rows = held([P, PACK, width], F32, f"y_rows{c}_{col0}", tag)
                y_rows.append(rows)
                for u, piece in enumerate(pieces(c)):
                    if piece[3] == col0:
                        nc.vector.tensor_tensor(
                            out=rows[:, piece[1] : piece[1] + piece[2], :],
                            in0=sums_of(top_banks[c], c, piece),
                            in1=damp[c][u][:],
                            op=MULT,
                        )
                nc.sync.dma_start(
                    out=out_0.rearrange("(p t) j -> p t j", t=PACK)[:, :, j0 + col0 : j0 + col0 + width], in_=rows[:]
                )
            y_round = []
            for (col0, width), rows in zip(spans, y_rows):
                y_round.append(held([P, width, PACK], BF16, f"y_round{c}_{col0}"))
                weave(y_round[-1][:], rows[:])
            for (col0, width), rounded in zip(spans, y_round):
                first = j0 + col0
                y_codes = held([P, width], U32, f"y_codes{c}_{col0}")
                quantize(y_codes[:], y_plane[:, first : first + width], rounded[:].rearrange("p j t -> p (j t)"))
                nc.sync.dma_start(
                    out=out_1[0].rearrange("p m t -> p (m t)")[:, PACK * first : PACK * (first + width)].bitcast(I32),
                    in_=y_codes[:].bitcast(I32),
                )

        steps = [(g, r) for g in range(len(ROUNDS)) for r in range(ROW_TILES)]

        def weave_z(n):
            g, r = steps[n]
            if r % PACK == PACK - 1:
                weave(z_round[g][r // PACK][:], z_rows[g, r // PACK][:])

        def multiply_z(n):
            g, r = steps[n]
            b = r // PACK
            if r % PACK == PACK - 1:
                quantize(z_codes[g][b][:], z_planes[g][b][:], z_round[g][b][:].rearrange("p j t -> p (j t)"))
            if r == ROW_TILES - 1:
                for c in range(len(CHUNKS)):
                    if ROUND_OF_CHUNK[c] == g:
                        second_stage(c, 0)
                        second_stage(c, 1)
                        damping(c)

        uppers = [pick_upper(*steps[0])]
        for n, (g, r) in enumerate(steps):
            if n + 1 < len(steps):
                uppers.append(pick_upper(*steps[n + 1]))
            pick_lower(g, r, uppers[n])
            if n >= 1:
                weave_z(n - 1)
            if n >= 2:
                multiply_z(n - 2)
        weave_z(len(steps) - 1)
        multiply_z(len(steps) - 1)

        for c, tag in enumerate(("z_round11", "damp01", None)):
            hand_out(c, tag)

        for quadrant in range(4):
            queue = nc.scalar if quadrant % 2 else nc.sync
            queue.dma_start(
                out=out_2[0, 4 * quadrant : 4 * quadrant + 4, :].bitcast(I32),
                in_=y_plane[32 * quadrant : 32 * quadrant + 4, :].bitcast(I32),
            )
